import numpy as np
import ml_dtypes


def mxq(x, axis, fmt="e4m3"):
    dtype, down = {"e4m3": (ml_dtypes.float8_e4m3fn, 7), "e5m2": (ml_dtypes.float8_e5m2, 14)}[fmt]
    v = np.moveaxis(np.asarray(x, np.float32).astype(ml_dtypes.bfloat16).astype(np.float64), axis, -1)
    blocks = v.reshape(v.shape[:-1] + (-1, 32))
    amax = np.abs(blocks).max(-1, keepdims=True)
    byte = np.maximum(np.where(amax > 0, np.frexp(amax)[1] - 1 + 127, 0) - down, 1)
    scale = np.exp2(byte - 127.0)
    codes = (blocks / scale).astype(np.float32).astype(dtype).astype(np.float64)
    return np.moveaxis((codes * scale).reshape(v.shape), -1, axis)


WIDE = False


def mx_kscale(k):
    if not WIDE:
        return np.ones(k)
    levels = np.array([10, -10, 5, -5, 0])
    if k % 512:
        return np.exp2(np.random.permutation(np.resize(levels, k // 32))).repeat(32)
    a = np.empty((k // 512, 16))
    for p in range(k // 512):
        a[p, :8] = np.random.permutation(np.resize(levels, 8))
        for g in range(8):
            far = levels[np.abs(levels - a[p, g]) >= 10]
            a[p, g + 8] = far[np.random.randint(len(far))]
    return np.exp2(a.ravel()).repeat(32)


def f64(x):
    return np.asarray(x).astype(np.float64)


def striped(idx):
    return np.tile(idx.reshape(-1, 16).T, (8, 1)).astype(np.uint16)


def unstriped(offs):
    return offs[:16].T.reshape(-1).astype(np.int64)


def pack_weight(w):
    k, n = w.shape
    w = f64(np.asarray(w, np.float32).astype(ml_dtypes.bfloat16)).reshape(k // 32, 32, n)
    amax = np.abs(w).max(1)
    byte = np.clip(np.where(amax > 0, np.frexp(amax)[1] - 1 + 127 - 7, 1), 1, 254)
    scaled = (w * np.exp2(127.0 - byte)[:, None, :]).reshape(k, n).astype(np.float32)
    words = np.ascontiguousarray(scaled.reshape(k // 512, 128, 4, n).transpose(0, 1, 3, 2)).astype(ml_dtypes.float8_e4m3fn).view(np.uint8)
    return words, np.ascontiguousarray(byte.astype(np.uint8).reshape(k // 512, 16, n))


def unpack_weight(words, scales):
    g, p, n, _ = words.shape
    vals = np.ascontiguousarray(words).view(ml_dtypes.float8_e4m3fn).astype(np.float64) * np.repeat(np.exp2(scales.astype(np.float64) - 127.0), 8, axis=1)[..., None]
    return vals.transpose(0, 1, 3, 2).reshape(g * 512, n)


def planes(y):
    n, m = y.shape
    v = y.astype(np.float32).astype(ml_dtypes.bfloat16).astype(np.float64).reshape(n // 32, 32, m)
    top = np.abs(v).max(1)
    byte = np.clip(np.where(top > 0, np.frexp(top)[1] - 1 + 127 - 7, 1), 1, 254)
    codes = (v * np.exp2(127.0 - byte)[:, None, :]).reshape(n, m).astype(np.float32).astype(ml_dtypes.float8_e4m3fn).view(np.uint8)
    words = codes.reshape(n // 512, 128, 4, m).transpose(0, 1, 3, 2)
    return np.ascontiguousarray(words), np.ascontiguousarray(byte.astype(np.uint8).reshape(n // 512, 16, m))


K, T, S, N, U = 1024, 1024, 512, 512, 1024


def setup_inputs():
    n = np.random.standard_normal
    s = mx_kscale(K)[:, None]
    packed_xT = pack_weight(n((K, T)) * s)
    return {
        "x_words": packed_xT[0],
        "x_scales": packed_xT[1],
        "mean": (n((N, U))).astype(np.float32),
        "var": (np.random.uniform(0.2, 2.0, (N, U))).astype(np.float32),
        "w1": (n((K, N)) / np.sqrt(K) / s).astype(np.float32),
        "w2": (n((K, N)) / np.sqrt(K) / s).astype(np.float32),
        "offs": striped(np.random.permutation(T)[:S]),
        "track": striped(np.random.permutation(U)[:S]),
    }


def reference(x_words, x_scales, mean, var, w1, w2, offs, track):
    mu = f64(mean)[:, unstriped(track)]
    va = f64(var)[:, unstriped(track)]
    xq = unpack_weight(x_words, x_scales)[:, unstriped(offs)]
    rr = np.exp(mxq(f64(w2), 0, "e4m3").T @ xq)
    dd = va + rr
    gain = va / dd
    y = mxq(f64(w1), 0, "e4m3").T @ xq
    out_0 = mu + gain * (y - mu)
    return (out_0,) + planes(out_0)

@@ -1,0 +1,215 @@
+from contextlib import ExitStack
+
+import concourse.mybir as mybir
+from concourse.masks import make_identity
+
+K, T, S, N, U = 1024, 1024, 512, 512, 1024
+FLOPS = 2 * 2 * K * N * S
+
+F32 = mybir.dt.float32
+BF16 = mybir.dt.bfloat16
+I32 = mybir.dt.int32
+U32 = mybir.dt.uint32
+U16 = mybir.dt.uint16
+U8 = mybir.dt.uint8
+FP8X4 = mybir.dt.float8_e4m3fn_x4
+ACT = mybir.ActivationFunctionType
+ALU = mybir.AluOpType
+
+P = 128
+PACK = 4
+K_PASS = P * PACK
+PASSES = K // K_PASS
+CH = S // P
+
+
+def tile_picked_ykal_mean_po_kernel(
+    tc, x_words, x_scales, mean, var, w1, w2, offs, track, out_0, out_1, out_2
+):
+    nc = tc.nc
+    with ExitStack() as ctx:
+        keep = ctx.enter_context(tc.tile_pool(name="keep", bufs=1))
+        psum = ctx.enter_context(tc.psum_pool(name="psum", bufs=1))
+
+        def sb(name, shape, dtype):
+            return keep.tile(shape, dtype, name=name, align_bytes=64)
+
+        def bank(name, b):
+            return psum.tile([P, PACK, P], F32, name=name, tag="bank%d" % b)
+
+        offs_t = keep.tile([P, S // 16], U16, name="offs_t")
+        track_t = keep.tile([P, S // 16], U16, name="track_t")
+        nc.sync.dma_start(track_t[:], track)
+
+        warm = sb("warm", [P, 2], F32)
+        nc.vector.memset(warm[:, 0:1], 1.0)
+        nc.scalar.activation(warm[:, 1:2], warm[:, 0:1], ACT.Ln)
+        ident = sb("ident", [P, P], F32)
+        make_identity(nc, ident[:])
+
+        xs = sb("xs", [P, T], U8)
+        nc.vector.memset(xs[:].bitcast(I32), 0)
+        for q in range(4):
+            nc.scalar.dma_start(xs[32 * q : 32 * q + 8, :].bitcast(I32), x_scales[:, 4 * q : 4 * q + 4, :].bitcast(I32))
+
+        def load_x(g):
+            t_ = sb("xw%d" % g, [P, T], U32)
+            nc.sync.dma_start(t_[:].bitcast(I32), x_words[g].rearrange("p n t -> p (n t)").bitcast(I32))
+            return t_
+
+        def load_w(w, name, g, c0, c1):
+            t_ = sb(name, [P, PACK, c1 - c0], F32)
+            nc.sync.dma_start(t_[:], w[g * K_PASS : (g + 1) * K_PASS, c0:c1].rearrange("(p j) n -> p j n", j=PACK))
+            return t_
+
+        def load_rows(src, name, t):
+            t_ = sb(name, [P, U], F32)
+            nc.sync.dma_start(t_[:], src.rearrange("(p t) u -> p t u", t=PACK)[:, t, :])
+            return t_
+
+        var_t = [load_rows(var, "var%d" % t, t) for t in range(2)]
+        nc.sync.dma_start(offs_t[:], offs)
+        var_t.extend([load_rows(var, "var%d" % t, t) for t in range(2, 4)])
+        xw0 = load_x(0)
+        xw1 = load_x(1)
+        w2a = load_w(w2, "w2a", 0, 0, N)
+        w2b = load_w(w2, "w2b", 1, 0, N)
+        mean_t = [load_rows(mean, "mean%d" % t, t) for t in range(2)]
+        w1a = load_w(w1, "w1a", 0, 0, N)
+        mean_t.extend([load_rows(mean, "mean%d" % t, t) for t in range(2, 4)])
+        w1b0 = load_w(w1, "w1b0", 1, 0, N // 2)
+        w1b1 = load_w(w1, "w1b1", 1, N // 2, N)
+
+        def gather(name, table):
+            t_ = sb(name, [P, S], F32)
+            nc.vector.tensor_copy(t_[:], table[:].indirect(track_t[:]))
+            return t_
+
+        lnva = []
+        for t in range(4):
+            va = gather("va%d" % t, var_t[t])
+            l_ = sb("ln%d" % t, [P, S], F32)
+            nc.scalar.activation(l_[:], va[:], ACT.Ln)
+            lnva.append(l_)
+
+        xg = []
+        for g, xw in enumerate((xw0, xw1)):
+            t_ = sb("xg%d" % g, [P, S], U32)
+            nc.vector.tensor_copy(t_[:], xw[:].indirect(offs_t[:]))
+            xg.append(t_)
+        xsg = sb("xsg", [P, S], U8)
+        nc.vector.tensor_copy(xsg[:], xs[:].indirect(offs_t[:]))
+
+        def cast(eng, dst, raw, m0, m1, t0):
+            o = dst[:, :, m0:m1, :].rearrange("p t m j -> p m j t")
+            i = raw[:].rearrange("p j (m t) -> p m j t", t=PACK)[:, :, :, t0 : t0 + 2]
+            if eng == "v":
+                nc.vector.tensor_copy(o, i)
+            else:
+                nc.scalar.copy(o, i)
+
+        def quant(name, pieces):
+            c_ = sb("%sc" % name, [P, N], U32)
+            s_ = sb("%ss" % name, [P, N], U8)
+            for h in range(2):
+                wb = sb("%sb%d" % (name, h), [P, 2, P, PACK], BF16)
+                for raw, m0, m1, engs in pieces:
+                    cast(engs[h], wb, raw, m0, m1, 2 * h)
+                cols = slice(2 * P * h, 2 * P * (h + 1))
+                nc.vector.quantize_mx(out=c_[:, cols].bitcast(FP8X4), scales=s_[:, cols], in_=wb[:].rearrange("p t m j -> p (t m j)"))
+            return c_, s_
+
+        def mm_z(acc, q, g, t):
+            cols = slice(t * P, (t + 1) * P)
+            nc.tensor.matmul_mx(
+                out=acc[:].rearrange("p c j -> p (c j)"),
+                lhsT=q[0][:, cols].bitcast(FP8X4),
+                lhsT_scale=q[1][:, cols],
+                rhs=xg[g][:].bitcast(FP8X4),
+                rhs_scale=xsg[4 * g : P, :],
+                start=(g == 0),
+                stop=(g == PASSES - 1),
+            )
+
+        def mm_y(acc, q, g, c):
+            cols = slice(c * P, (c + 1) * P)
+            nc.tensor.matmul_mx(
+                out=acc[:].rearrange("p t m -> p (t m)"),
+                lhsT=xg[g][:, cols].bitcast(FP8X4),
+                lhsT_scale=xsg[4 * g : P, cols],
+                rhs=q[0][:].bitcast(FP8X4),
+                rhs_scale=q[1][:],
+                start=(g == 0),
+                stop=(g == PASSES - 1),
+            )
+
+        def turn(out, src, start, stop):
+            nc.tensor.matmul(out, src, ident[:], start=start, stop=stop, is_transpose=True)
+
+        zb = [bank("z%d" % t, t) for t in range(4)]
+        q = quant("w2a", [(w2a, 0, P, "vs")])
+        for t in range(4):
+            mm_z(zb[t], q, 0, t)
+        q = quant("w2b", [(w2b, 0, P, "vs")])
+        for t in range(4):
+            mm_z(zb[t], q, 1, t)
+
+        gT = sb("gT", [P, PACK, CH, P], F32)
+        for t in range(4):
+            nz = sb("nz%d" % t, [P, CH, P], F32)
+            nc.scalar.activation(nz[:], zb[t][:], ACT.Copy, scale=-1.0)
+            ab = bank("a%d" % t, 4 + t)
+            for c in range(CH):
+                turn(ab[:, c, :], lnva[t][:, c * P : (c + 1) * P], True, False)
+                turn(ab[:, c, :], nz[:, c, :], False, True)
+            nc.scalar.activation(gT[:, t, :, :], ab[:], ACT.Sigmoid)
+
+        rest = []
+
+        def mean_part(t):
+            mu = gather("mu%d" % t, mean_t[t])
+            mb = bank("m%d" % t, t)
+            for c in range(CH):
+                turn(mb[:, c, :], mu[:, c * P : (c + 1) * P], True, True)
+            r_ = sb("r%d" % t, [P, CH, P], F32)
+            nc.vector.scalar_tensor_tensor(r_[:], gT[:, t, :, :], 1.0, mb[:], ALU.subtract, ALU.mult)
+            rest.append(r_)
+
+        mean_part(0)
+        mean_part(1)
+        qa = quant("w1a", [(w1a, 0, P, "vs")])
+        mean_part(2)
+        mean_part(3)
+        ob = [bank("o%d" % c, 4 + c) for c in range(CH)]
+        for t in range(4):
+            for c in range(CH):
+                turn(ob[c][:, t, :], rest[t][:, c, :], t == 0, False)
+        yb = [bank("y%d" % c, c) for c in range(CH)]
+        for c in range(CH):
+            mm_y(yb[c], qa, 0, c)
+        qb = quant("w1b", [(w1b0, 0, P // 2, "ss"), (w1b1, P // 2, P, "vs")])
+        for c in range(CH):
+            mm_y(yb[c], qb, 1, c)
+
+        out_rows = out_0.rearrange("(p t) s -> p t s", t=PACK)
+        oc = sb("oc", [P, S], U32)
+        osc = sb("osc", [P, S], U8)
+        words = out_1[0].rearrange("p c r -> p (c r)").bitcast(I32)
+        for c in range(CH):
+            p_ = sb("p%d" % c, [P, PACK, P], F32)
+            nc.vector.scalar_tensor_tensor(p_[:], gT[:, :, c, :], -1.0, yb[c][:], ALU.mult, ALU.mult)
+            for t in range(4):
+                turn(ob[c][:, t, :], p_[:, t, :], False, t == 3)
+        for c in range(CH):
+            cols = slice(c * P, (c + 1) * P)
+            res = sb("res%d" % c, [P, PACK, P], F32)
+            nc.scalar.activation(res[:], ob[c][:], ACT.Copy, scale=-1.0)
+            nc.sync.dma_start(out_rows[:, :, cols], res[:])
+            rb = sb("rb%d" % c, [P, P, PACK], BF16)
+            nc.vector.tensor_copy(rb[:].rearrange("p (c i) t -> p c t i", i=4), res[:].rearrange("p t (c i) -> p c t i", i=4))
+            nc.vector.quantize_mx(out=oc[:, cols].bitcast(FP8X4), scales=osc[:, cols], in_=rb[:].rearrange("p c t -> p (c t)"))
+        nc.sync.dma_start(words[:, : 3 * P], oc[:, : 3 * P].bitcast(I32))
+        nc.sync.dma_start(words[:, 3 * P :], oc[:, 3 * P :].bitcast(I32))
+        for qd in range(4):
+            eng = nc.scalar if qd % 2 == 0 else nc.sync
+            eng.dma_start(out_2[0, 4 * qd : 4 * qd + 4, :].bitcast(I32), osc[32 * qd : 32 * qd + 4, :].bitcast(I32))

@@ -1,7 +1,6 @@
 from contextlib import ExitStack
 
 import concourse.mybir as mybir
-from concourse.masks import make_identity
 
 K, T, S, N, U = 1024, 1024, 512, 512, 1024
 FLOPS = 2 * 2 * K * N * S
@@ -20,7 +19,8 @@ P = 128
 PACK = 4
 K_PASS = P * PACK
 PASSES = K // K_PASS
-CH = S // P
+HALF = S // 2
+V_COLS = 176
 
 
 def tile_picked_ykal_mean_po_kernel(
@@ -34,32 +34,25 @@ def tile_picked_ykal_mean_po_kernel(
         def sb(name, shape, dtype):
             return keep.tile(shape, dtype, name=name, align_bytes=64)
 
-        def bank(name, b):
-            return psum.tile([P, PACK, P], F32, name=name, tag="bank%d" % b)
-
         offs_t = keep.tile([P, S // 16], U16, name="offs_t")
         track_t = keep.tile([P, S // 16], U16, name="track_t")
         nc.sync.dma_start(track_t[:], track)
 
-        warm = sb("warm", [P, 2], F32)
-        nc.vector.memset(warm[:, 0:1], 1.0)
-        nc.scalar.activation(warm[:, 1:2], warm[:, 0:1], ACT.Ln)
-        ident = sb("ident", [P, P], F32)
-        make_identity(nc, ident[:])
-
         xs = sb("xs", [P, T], U8)
         nc.vector.memset(xs[:].bitcast(I32), 0)
-        for q in range(4):
-            nc.scalar.dma_start(xs[32 * q : 32 * q + 8, :].bitcast(I32), x_scales[:, 4 * q : 4 * q + 4, :].bitcast(I32))
+
+        warm = sb("warm", [P, 4], F32)
+        nc.vector.memset(warm[:, 0:1], 1.0)
+        nc.scalar.activation(warm[:, 1:2], warm[:, 0:1], ACT.Ln)
 
         def load_x(g):
             t_ = sb("xw%d" % g, [P, T], U32)
             nc.sync.dma_start(t_[:].bitcast(I32), x_words[g].rearrange("p n t -> p (n t)").bitcast(I32))
             return t_
 
-        def load_w(w, name, g, c0, c1):
-            t_ = sb(name, [P, PACK, c1 - c0], F32)
-            nc.sync.dma_start(t_[:], w[g * K_PASS : (g + 1) * K_PASS, c0:c1].rearrange("(p j) n -> p j n", j=PACK))
+        def load_w(w, name, g):
+            t_ = sb(name, [P, PACK, N], F32)
+            nc.sync.dma_start(t_[:], w[g * K_PASS : (g + 1) * K_PASS, :].rearrange("(p j) n -> p j n", j=PACK))
             return t_
 
         def load_rows(src, name, t):
@@ -69,147 +62,147 @@ def tile_picked_ykal_mean_po_kernel(
 
         var_t = [load_rows(var, "var%d" % t, t) for t in range(2)]
         nc.sync.dma_start(offs_t[:], offs)
-        var_t.extend([load_rows(var, "var%d" % t, t) for t in range(2, 4)])
+        for q in range(4):
+            nc.sync.dma_start(xs[32 * q : 32 * q + 8, :].bitcast(I32), x_scales[:, 4 * q : 4 * q + 4, :].bitcast(I32))
+        var_t.append(load_rows(var, "var2", 2))
         xw0 = load_x(0)
+        w2a = load_w(w2, "w2a", 0)
+        var_t.append(load_rows(var, "var3", 3))
         xw1 = load_x(1)
-        w2a = load_w(w2, "w2a", 0, 0, N)
-        w2b = load_w(w2, "w2b", 1, 0, N)
-        mean_t = [load_rows(mean, "mean%d" % t, t) for t in range(2)]
-        w1a = load_w(w1, "w1a", 0, 0, N)
-        mean_t.extend([load_rows(mean, "mean%d" % t, t) for t in range(2, 4)])
-        w1b0 = load_w(w1, "w1b0", 1, 0, N // 2)
-        w1b1 = load_w(w1, "w1b1", 1, N // 2, N)
-
-        def gather(name, table):
-            t_ = sb(name, [P, S], F32)
-            nc.vector.tensor_copy(t_[:], table[:].indirect(track_t[:]))
-            return t_
+        w2b = load_w(w2, "w2b", 1)
+        w1a = load_w(w1, "w1a", 0)
+        mean_t = [load_rows(mean, "mean%d" % t, t) for t in range(3)]
+        w1b = load_w(w1, "w1b", 1)
+        mean_t.append(load_rows(mean, "mean3", 3))
 
         lnva = []
-        for t in range(4):
-            va = gather("va%d" % t, var_t[t])
+
+        def var_part(t):
+            va = sb("va%d" % t, [P, S], F32)
+            nc.vector.tensor_copy(va[:], var_t[t][:].indirect(track_t[:]))
             l_ = sb("ln%d" % t, [P, S], F32)
             nc.scalar.activation(l_[:], va[:], ACT.Ln)
             lnva.append(l_)
+            return va
 
         xg = []
-        for g, xw in enumerate((xw0, xw1)):
+
+        def x_part(g, xw):
             t_ = sb("xg%d" % g, [P, S], U32)
             nc.vector.tensor_copy(t_[:], xw[:].indirect(offs_t[:]))
             xg.append(t_)
+
+        for t in range(3):
+            var_part(t)
+        x_part(0, xw0)
         xsg = sb("xsg", [P, S], U8)
         nc.vector.tensor_copy(xsg[:], xs[:].indirect(offs_t[:]))
 
-        def cast(eng, dst, raw, m0, m1, t0):
-            o = dst[:, :, m0:m1, :].rearrange("p t m j -> p m j t")
-            i = raw[:].rearrange("p j (m t) -> p m j t", t=PACK)[:, :, :, t0 : t0 + 2]
-            if eng == "v":
-                nc.vector.tensor_copy(o, i)
-            else:
-                nc.scalar.copy(o, i)
+        last = []
 
-        def quant(name, pieces):
-            c_ = sb("%sc" % name, [P, N], U32)
-            s_ = sb("%ss" % name, [P, N], U8)
-            for h in range(2):
-                wb = sb("%sb%d" % (name, h), [P, 2, P, PACK], BF16)
-                for raw, m0, m1, engs in pieces:
-                    cast(engs[h], wb, raw, m0, m1, 2 * h)
-                cols = slice(2 * P * h, 2 * P * (h + 1))
-                nc.vector.quantize_mx(out=c_[:, cols].bitcast(FP8X4), scales=s_[:, cols], in_=wb[:].rearrange("p t m j -> p (t m j)"))
-            return c_, s_
+        def quant(name, raw, parts):
+            staged = []
+            for t0, t1, eng in parts:
+                wb = sb("%sb%d" % (name, t0), [P, t1 - t0, P, PACK], BF16)
+                o = wb[:].rearrange("p t m j -> p m j t")
+                i = raw[:].rearrange("p j (m t) -> p m j t", t=PACK)[:, :, :, t0:t1]
+                if eng == "v":
+                    nc.vector.tensor_copy(o, i)
+                else:
+                    nc.scalar.copy(o, i)
+                staged.append(wb)
+            last.append(staged[-1])
+            res_ = []
+            for (t0, t1, eng), wb in zip(parts, staged):
+                c_ = sb("%sc%d" % (name, t0), [P, (t1 - t0) * P], U32)
+                s_ = sb("%ss%d" % (name, t0), [P, (t1 - t0) * P], U8)
+                nc.vector.quantize_mx(out=c_[:].bitcast(FP8X4), scales=s_[:], in_=wb[:].rearrange("p t m j -> p (t m j)"))
+                for t in range(t0, t1):
+                    cols = slice((t - t0) * P, (t - t0 + 1) * P)
+                    res_.append((c_[:, cols], s_[:, cols]))
+            return res_
 
-        def mm_z(acc, q, g, t):
-            cols = slice(t * P, (t + 1) * P)
+        def mm(acc, q, g):
             nc.tensor.matmul_mx(
-                out=acc[:].rearrange("p c j -> p (c j)"),
-                lhsT=q[0][:, cols].bitcast(FP8X4),
-                lhsT_scale=q[1][:, cols],
+                out=acc[:],
+                lhsT=q[0].bitcast(FP8X4),
+                lhsT_scale=q[1],
                 rhs=xg[g][:].bitcast(FP8X4),
                 rhs_scale=xsg[4 * g : P, :],
                 start=(g == 0),
                 stop=(g == PASSES - 1),
             )
 
-        def mm_y(acc, q, g, c):
-            cols = slice(c * P, (c + 1) * P)
-            nc.tensor.matmul_mx(
-                out=acc[:].rearrange("p t m -> p (t m)"),
-                lhsT=xg[g][:, cols].bitcast(FP8X4),
-                lhsT_scale=xsg[4 * g : P, cols],
-                rhs=q[0][:].bitcast(FP8X4),
-                rhs_scale=q[1][:],
-                start=(g == 0),
-                stop=(g == PASSES - 1),
-            )
+        zb = [psum.tile([P, S], F32, name="z%d" % t) for t in range(4)]
+        yb = [psum.tile([P, S], F32, name="y%d" % t) for t in range(4)]
 
-        def turn(out, src, start, stop):
-            nc.tensor.matmul(out, src, ident[:], start=start, stop=stop, is_transpose=True)
-
-        zb = [bank("z%d" % t, t) for t in range(4)]
-        q = quant("w2a", [(w2a, 0, P, "vs")])
+        q = quant("w2a", w2a, [(0, 2, "s"), (2, 4, "s")])
         for t in range(4):
-            mm_z(zb[t], q, 0, t)
-        q = quant("w2b", [(w2b, 0, P, "vs")])
+            mm(zb[t], q[t], 0)
+        va3 = var_part(3)
+        x_part(1, xw1)
+        q = quant("w2b", w2b, [(0, 2, "v"), (2, 4, "s")])
+        nc.scalar.activation(warm[:, 2:3], last[-1][:, 0, 0, 0:1], ACT.Sigmoid)
         for t in range(4):
-            mm_z(zb[t], q, 1, t)
-
-        gT = sb("gT", [P, PACK, CH, P], F32)
+            mm(zb[t], q[t], 1)
+        keepw = []
         for t in range(4):
-            nz = sb("nz%d" % t, [P, CH, P], F32)
-            nc.scalar.activation(nz[:], zb[t][:], ACT.Copy, scale=-1.0)
-            ab = bank("a%d" % t, 4 + t)
-            for c in range(CH):
-                turn(ab[:, c, :], lnva[t][:, c * P : (c + 1) * P], True, False)
-                turn(ab[:, c, :], nz[:, c, :], False, True)
-            nc.scalar.activation(gT[:, t, :, :], ab[:], ACT.Sigmoid)
-
+            a_ = sb("a%d" % t, [P, S], F32)
+            nc.vector.tensor_tensor(a_[:], zb[t][:], lnva[t][:], ALU.subtract)
+            h_ = sb("h%d" % t, [P, S], F32)
+            nc.scalar.activation(h_[:], a_[:], ACT.Sigmoid)
+            keepw.append(h_)
+        q = quant("w1a", w1a, [(0, 2, "s"), (2, 4, "s")])
         rest = []
 
         def mean_part(t):
-            mu = gather("mu%d" % t, mean_t[t])
-            mb = bank("m%d" % t, t)
-            for c in range(CH):
-                turn(mb[:, c, :], mu[:, c * P : (c + 1) * P], True, True)
-            r_ = sb("r%d" % t, [P, CH, P], F32)
-            nc.vector.scalar_tensor_tensor(r_[:], gT[:, t, :, :], 1.0, mb[:], ALU.subtract, ALU.mult)
+            r_ = sb("r%d" % t, [P, S], F32)
+            nc.vector.tensor_tensor(r_[:], mean_t[t][:].indirect(track_t[:]), keepw[t][:], ALU.mult)
             rest.append(r_)
 
-        mean_part(0)
-        mean_part(1)
-        qa = quant("w1a", [(w1a, 0, P, "vs")])
-        mean_part(2)
-        mean_part(3)
-        ob = [bank("o%d" % c, 4 + c) for c in range(CH)]
         for t in range(4):
-            for c in range(CH):
-                turn(ob[c][:, t, :], rest[t][:, c, :], t == 0, False)
-        yb = [bank("y%d" % c, c) for c in range(CH)]
-        for c in range(CH):
-            mm_y(yb[c], qa, 0, c)
-        qb = quant("w1b", [(w1b0, 0, P // 2, "ss"), (w1b1, P // 2, P, "vs")])
-        for c in range(CH):
-            mm_y(yb[c], qb, 1, c)
+            mm(yb[t], q[t], 0)
+        for t in range(3):
+            mean_part(t)
+        q = quant("w1b", w1b, [(0, 2, "s"), (2, 4, "s")])
+        for t in range(4):
+            mm(yb[t], q[t], 1)
+        mean_part(3)
 
         out_rows = out_0.rearrange("(p t) s -> p t s", t=PACK)
+        words = out_1[0].rearrange("p c r -> p (c r)").bitcast(I32)
         oc = sb("oc", [P, S], U32)
         osc = sb("osc", [P, S], U8)
-        words = out_1[0].rearrange("p c r -> p (c r)").bitcast(I32)
-        for c in range(CH):
-            p_ = sb("p%d" % c, [P, PACK, P], F32)
-            nc.vector.scalar_tensor_tensor(p_[:], gT[:, :, c, :], -1.0, yb[c][:], ALU.mult, ALU.mult)
+        staged = []
+        for h in range(2):
+            cols = slice(h * HALF, (h + 1) * HALF)
+            res = sb("res%d" % h, [P, PACK, HALF], F32)
+            prods = []
             for t in range(4):
-                turn(ob[c][:, t, :], p_[:, t, :], False, t == 3)
-        for c in range(CH):
-            cols = slice(c * P, (c + 1) * P)
-            res = sb("res%d" % c, [P, PACK, P], F32)
-            nc.scalar.activation(res[:], ob[c][:], ACT.Copy, scale=-1.0)
-            nc.sync.dma_start(out_rows[:, :, cols], res[:])
-            rb = sb("rb%d" % c, [P, P, PACK], BF16)
-            nc.vector.tensor_copy(rb[:].rearrange("p (c i) t -> p c t i", i=4), res[:].rearrange("p t (c i) -> p c t i", i=4))
-            nc.vector.quantize_mx(out=oc[:, cols].bitcast(FP8X4), scales=osc[:, cols], in_=rb[:].rearrange("p c t -> p (c t)"))
-        nc.sync.dma_start(words[:, : 3 * P], oc[:, : 3 * P].bitcast(I32))
-        nc.sync.dma_start(words[:, 3 * P :], oc[:, 3 * P :].bitcast(I32))
+                p_ = sb("p%d%d" % (h, t), [P, HALF], F32)
+                nc.vector.scalar_tensor_tensor(p_[:], keepw[t][:, cols], 1.0, yb[t][:, cols], ALU.subtract, ALU.mult)
+                prods.append(p_)
+            for t in range(4):
+                nc.vector.tensor_tensor(res[:, t, :], rest[t][:, cols], prods[t][:], ALU.subtract)
+                if h == 1:
+                    nc.sync.dma_start(out_rows[:, t, cols], res[:, t, :])
+            if h == 0:
+                nc.sync.dma_start(out_rows[:, :, cols], res[:])
+            rb = sb("rb%d" % h, [P, HALF, PACK], BF16)
+            o = rb[:].rearrange("p (c i) t -> p c t i", i=4)
+            i = res[:].rearrange("p t (c i) -> p c t i", i=4)
+            if h == 0:
+                nc.scalar.copy(o, i)
+            else:
+                nc.vector.tensor_copy(o[:, : V_COLS // 4], i[:, : V_COLS // 4])
+                nc.scalar.copy(o[:, V_COLS // 4 :], i[:, V_COLS // 4 :])
+            staged.append(rb)
+        for h in range(2):
+            cols = slice(h * HALF, (h + 1) * HALF)
+            nc.vector.quantize_mx(out=oc[:, cols].bitcast(FP8X4), scales=osc[:, cols], in_=staged[h][:].rearrange("p c t -> p (c t)"))
+            if h == 0:
+                nc.sync.dma_start(words[:, cols], oc[:, cols].bitcast(I32))
         for qd in range(4):
             eng = nc.scalar if qd % 2 == 0 else nc.sync
             eng.dma_start(out_2[0, 4 * qd : 4 * qd + 4, :].bitcast(I32), osc[32 * qd : 32 * qd + 4, :].bitcast(I32))
+        nc.scalar.dma_start(words[:, HALF:], oc[:, HALF:].bitcast(I32))

@@ -20,7 +20,7 @@ PACK = 4
 K_PASS = P * PACK
 PASSES = K // K_PASS
 HALF = S // 2
-V_COLS = 176
+V_COLS = 144
 
 
 def tile_picked_ykal_mean_po_kernel(
@@ -41,9 +41,6 @@ def tile_picked_ykal_mean_po_kernel(
         xs = sb("xs", [P, T], U8)
         nc.vector.memset(xs[:].bitcast(I32), 0)
 
-        warm = sb("warm", [P, 4], F32)
-        nc.vector.memset(warm[:, 0:1], 1.0)
-        nc.scalar.activation(warm[:, 1:2], warm[:, 0:1], ACT.Ln)
 
         def load_x(g):
             t_ = sb("xw%d" % g, [P, T], U32)
@@ -70,8 +67,9 @@ def tile_picked_ykal_mean_po_kernel(
         var_t.append(load_rows(var, "var3", 3))
         xw1 = load_x(1)
         w2b = load_w(w2, "w2b", 1)
+        mean_t = [load_rows(mean, "mean0", 0)]
         w1a = load_w(w1, "w1a", 0)
-        mean_t = [load_rows(mean, "mean%d" % t, t) for t in range(3)]
+        mean_t.extend([load_rows(mean, "mean%d" % t, t) for t in range(1, 3)])
         w1b = load_w(w1, "w1b", 1)
         mean_t.append(load_rows(mean, "mean3", 3))
 
@@ -98,8 +96,6 @@ def tile_picked_ykal_mean_po_kernel(
         xsg = sb("xsg", [P, S], U8)
         nc.vector.tensor_copy(xsg[:], xs[:].indirect(offs_t[:]))
 
-        last = []
-
         def quant(name, raw, parts):
             staged = []
             for t0, t1, eng in parts:
@@ -111,7 +107,6 @@ def tile_picked_ykal_mean_po_kernel(
                 else:
                     nc.scalar.copy(o, i)
                 staged.append(wb)
-            last.append(staged[-1])
             res_ = []
             for (t0, t1, eng), wb in zip(parts, staged):
                 c_ = sb("%sc%d" % (name, t0), [P, (t1 - t0) * P], U32)
@@ -136,15 +131,16 @@ def tile_picked_ykal_mean_po_kernel(
         zb = [psum.tile([P, S], F32, name="z%d" % t) for t in range(4)]
         yb = [psum.tile([P, S], F32, name="y%d" % t) for t in range(4)]
 
-        q = quant("w2a", w2a, [(0, 2, "s"), (2, 4, "s")])
+        q = quant("w2a", w2a, [(0, 2, "v"), (2, 4, "s")])
         for t in range(4):
             mm(zb[t], q[t], 0)
-        va3 = var_part(3)
+        var_part(3)
         x_part(1, xw1)
         q = quant("w2b", w2b, [(0, 2, "v"), (2, 4, "s")])
-        nc.scalar.activation(warm[:, 2:3], last[-1][:, 0, 0, 0:1], ACT.Sigmoid)
         for t in range(4):
             mm(zb[t], q[t], 1)
+        mu0 = sb("mu0", [P, S], F32)
+        nc.vector.tensor_copy(mu0[:], mean_t[0][:].indirect(track_t[:]))
         keepw = []
         for t in range(4):
             a_ = sb("a%d" % t, [P, S], F32)
@@ -152,18 +148,19 @@ def tile_picked_ykal_mean_po_kernel(
             h_ = sb("h%d" % t, [P, S], F32)
             nc.scalar.activation(h_[:], a_[:], ACT.Sigmoid)
             keepw.append(h_)
-        q = quant("w1a", w1a, [(0, 2, "s"), (2, 4, "s")])
         rest = []
 
         def mean_part(t):
             r_ = sb("r%d" % t, [P, S], F32)
-            nc.vector.tensor_tensor(r_[:], mean_t[t][:].indirect(track_t[:]), keepw[t][:], ALU.mult)
+            nc.vector.tensor_tensor(r_[:], mu0[:] if t == 0 else mean_t[t][:].indirect(track_t[:]), keepw[t][:], ALU.mult)
             rest.append(r_)
 
+        for t in range(2):
+            mean_part(t)
+        q = quant("w1a", w1a, [(0, 2, "s"), (2, 4, "s")])
         for t in range(4):
             mm(yb[t], q[t], 0)
-        for t in range(3):
-            mean_part(t)
+        mean_part(2)
         q = quant("w1b", w1b, [(0, 2, "s"), (2, 4, "s")])
         for t in range(4):
             mm(yb[t], q[t], 1)
@@ -174,20 +171,22 @@ def tile_picked_ykal_mean_po_kernel(
         oc = sb("oc", [P, S], U32)
         osc = sb("osc", [P, S], U8)
         staged = []
+        prods = {}
+        for pair in range(2):
+            for h in range(2):
+                cols = slice(h * HALF, (h + 1) * HALF)
+                for t in (2 * pair, 2 * pair + 1):
+                    p_ = sb("p%d%d" % (h, t), [P, HALF], F32)
+                    nc.vector.scalar_tensor_tensor(p_[:], keepw[t][:, cols], 1.0, yb[t][:, cols], ALU.subtract, ALU.mult)
+                    prods[(h, t)] = p_
         for h in range(2):
             cols = slice(h * HALF, (h + 1) * HALF)
             res = sb("res%d" % h, [P, PACK, HALF], F32)
-            prods = []
             for t in range(4):
-                p_ = sb("p%d%d" % (h, t), [P, HALF], F32)
-                nc.vector.scalar_tensor_tensor(p_[:], keepw[t][:, cols], 1.0, yb[t][:, cols], ALU.subtract, ALU.mult)
-                prods.append(p_)
-            for t in range(4):
-                nc.vector.tensor_tensor(res[:, t, :], rest[t][:, cols], prods[t][:], ALU.subtract)
-                if h == 1:
-                    nc.sync.dma_start(out_rows[:, t, cols], res[:, t, :])
-            if h == 0:
-                nc.sync.dma_start(out_rows[:, :, cols], res[:])
+                eng = nc.gpsimd if h == 0 and t < 3 else nc.vector
+                eng.tensor_tensor(res[:, t, :], rest[t][:, cols], prods[(h, t)][:], ALU.subtract)
+                if t % 2 == 1:
+                    nc.sync.dma_start(out_rows[:, t - 1 : t + 1, cols], res[:, t - 1 : t + 1, :])
             rb = sb("rb%d" % h, [P, HALF, PACK], BF16)
             o = rb[:].rearrange("p (c i) t -> p c t i", i=4)
             i = res[:].rearrange("p t (c i) -> p c t i", i=4)
@@ -202,7 +201,7 @@ def tile_picked_ykal_mean_po_kernel(
             nc.vector.quantize_mx(out=oc[:, cols].bitcast(FP8X4), scales=osc[:, cols], in_=staged[h][:].rearrange("p c t -> p (c t)"))
             if h == 0:
                 nc.sync.dma_start(words[:, cols], oc[:, cols].bitcast(I32))
+        nc.sync.dma_start(words[:, HALF:], oc[:, HALF:].bitcast(I32))
         for qd in range(4):
-            eng = nc.scalar if qd % 2 == 0 else nc.sync
+            eng = nc.sync if qd == 3 else nc.scalar
             eng.dma_start(out_2[0, 4 * qd : 4 * qd + 4, :].bitcast(I32), osc[32 * qd : 32 * qd + 4, :].bitcast(I32))
-        nc.scalar.dma_start(words[:, HALF:], oc[:, HALF:].bitcast(I32))

@@ -36,7 +36,6 @@ def tile_picked_ykal_mean_po_kernel(
 
         offs_t = keep.tile([P, S // 16], U16, name="offs_t")
         track_t = keep.tile([P, S // 16], U16, name="track_t")
-        nc.sync.dma_start(track_t[:], track)
 
         xs = sb("xs", [P, T], U8)
         nc.vector.memset(xs[:].bitcast(I32), 0)
@@ -57,14 +56,18 @@ def tile_picked_ykal_mean_po_kernel(
             nc.sync.dma_start(t_[:], src.rearrange("(p t) u -> p t u", t=PACK)[:, t, :])
             return t_
 
-        var_t = [load_rows(var, "var%d" % t, t) for t in range(2)]
+        def load_pair(t):
+            t_ = sb("var%d" % t, [P, 2, U], F32)
+            nc.sync.dma_start(t_[:], var.rearrange("(p t) u -> p t u", t=PACK)[:, t : t + 2, :])
+            return [t_[:, 0, :], t_[:, 1, :]]
+
         nc.sync.dma_start(offs_t[:], offs)
+        xw0 = load_x(0)
+        nc.sync.dma_start(track_t[:], track)
         for q in range(4):
             nc.sync.dma_start(xs[32 * q : 32 * q + 8, :].bitcast(I32), x_scales[:, 4 * q : 4 * q + 4, :].bitcast(I32))
-        var_t.append(load_rows(var, "var2", 2))
-        xw0 = load_x(0)
+        var_t = load_pair(0) + load_pair(2)
         w2a = load_w(w2, "w2a", 0)
-        var_t.append(load_rows(var, "var3", 3))
         xw1 = load_x(1)
         w2b = load_w(w2, "w2b", 1)
         mean_t = [load_rows(mean, "mean0", 0)]
@@ -77,7 +80,7 @@ def tile_picked_ykal_mean_po_kernel(
 
         def var_part(t):
             va = sb("va%d" % t, [P, S], F32)
-            nc.vector.tensor_copy(va[:], var_t[t][:].indirect(track_t[:]))
+            nc.vector.tensor_copy(va[:], var_t[t].indirect(track_t[:]))
             l_ = sb("ln%d" % t, [P, S], F32)
             nc.scalar.activation(l_[:], va[:], ACT.Ln)
             lnva.append(l_)
@@ -90,32 +93,33 @@ def tile_picked_ykal_mean_po_kernel(
             nc.vector.tensor_copy(t_[:], xw[:].indirect(offs_t[:]))
             xg.append(t_)
 
-        for t in range(3):
-            var_part(t)
         x_part(0, xw0)
         xsg = sb("xsg", [P, S], U8)
         nc.vector.tensor_copy(xsg[:], xs[:].indirect(offs_t[:]))
+        for t in range(4):
+            var_part(t)
 
-        def quant(name, raw, parts):
+        def cast(eng, dst, raw, m0, m1, t0, t1):
+            o = dst[:, :, m0:m1, :].rearrange("p t m j -> p m j t")
+            i = raw[:].rearrange("p j (m t) -> p m j t", t=PACK)[:, m0:m1, :, t0:t1]
+            if eng == "v":
+                nc.vector.tensor_copy(o, i)
+            else:
+                nc.scalar.copy(o, i)
+
+        def quant_tiles(name, src, n_tiles):
+            c_ = sb("%sc" % name, [P, n_tiles * P], U32)
+            s_ = sb("%ss" % name, [P, n_tiles * P], U8)
+            nc.vector.quantize_mx(out=c_[:].bitcast(FP8X4), scales=s_[:], in_=src.rearrange("p t m j -> p (t m j)"))
+            return [(c_[:, t * P : (t + 1) * P], s_[:, t * P : (t + 1) * P]) for t in range(n_tiles)]
+
+        def quant_pairs(name, raw, engines):
             staged = []
-            for t0, t1, eng in parts:
-                wb = sb("%sb%d" % (name, t0), [P, t1 - t0, P, PACK], BF16)
-                o = wb[:].rearrange("p t m j -> p m j t")
-                i = raw[:].rearrange("p j (m t) -> p m j t", t=PACK)[:, :, :, t0:t1]
-                if eng == "v":
-                    nc.vector.tensor_copy(o, i)
-                else:
-                    nc.scalar.copy(o, i)
+            for t0, eng in zip((0, 2), engines):
+                wb = sb("%sb%d" % (name, t0), [P, 2, P, PACK], BF16)
+                cast(eng, wb, raw, 0, P, t0, t0 + 2)
                 staged.append(wb)
-            res_ = []
-            for (t0, t1, eng), wb in zip(parts, staged):
-                c_ = sb("%sc%d" % (name, t0), [P, (t1 - t0) * P], U32)
-                s_ = sb("%ss%d" % (name, t0), [P, (t1 - t0) * P], U8)
-                nc.vector.quantize_mx(out=c_[:].bitcast(FP8X4), scales=s_[:], in_=wb[:].rearrange("p t m j -> p (t m j)"))
-                for t in range(t0, t1):
-                    cols = slice((t - t0) * P, (t - t0 + 1) * P)
-                    res_.append((c_[:, cols], s_[:, cols]))
-            return res_
+            return quant_tiles(name + "0", staged[0][:], 2) + quant_tiles(name + "1", staged[1][:], 2)
 
         def mm(acc, q, g):
             nc.tensor.matmul_mx(
@@ -131,21 +135,25 @@ def tile_picked_ykal_mean_po_kernel(
         zb = [psum.tile([P, S], F32, name="z%d" % t) for t in range(4)]
         yb = [psum.tile([P, S], F32, name="y%d" % t) for t in range(4)]
 
-        q = quant("w2a", w2a, [(0, 2, "v"), (2, 4, "s")])
+        q = quant_pairs("w2a", w2a, "vs")
         for t in range(4):
             mm(zb[t], q[t], 0)
-        var_part(3)
         x_part(1, xw1)
-        q = quant("w2b", w2b, [(0, 2, "v"), (2, 4, "s")])
+        q = quant_pairs("w2b", w2b, "vs")
         for t in range(4):
             mm(zb[t], q[t], 1)
         mu0 = sb("mu0", [P, S], F32)
         nc.vector.tensor_copy(mu0[:], mean_t[0][:].indirect(track_t[:]))
         keepw = []
+        w1a_b = sb("w1ab", [P, PACK, P, PACK], BF16)
         for t in range(4):
             a_ = sb("a%d" % t, [P, S], F32)
             nc.vector.tensor_tensor(a_[:], zb[t][:], lnva[t][:], ALU.subtract)
-            h_ = sb("h%d" % t, [P, S], F32)
+            if t == 2:
+                cast("s", w1a_b, w1a, 0, P, 0, 4)
+                h_ = keep.tile([P, S], F32, name="h2", tag="w1a", align_bytes=64)
+            else:
+                h_ = sb("h%d" % t, [P, S], F32)
             nc.scalar.activation(h_[:], a_[:], ACT.Sigmoid)
             keepw.append(h_)
         rest = []
@@ -157,11 +165,11 @@ def tile_picked_ykal_mean_po_kernel(
 
         for t in range(2):
             mean_part(t)
-        q = quant("w1a", w1a, [(0, 2, "s"), (2, 4, "s")])
+        q = quant_tiles("w1a", w1a_b[:], 4)
         for t in range(4):
             mm(yb[t], q[t], 0)
         mean_part(2)
-        q = quant("w1b", w1b, [(0, 2, "s"), (2, 4, "s")])
+        q = quant_pairs("w1b", w1b, "ss")
         for t in range(4):
             mm(yb[t], q[t], 1)
         mean_part(3)

@@ -19,8 +19,11 @@ P = 128
 PACK = 4
 K_PASS = P * PACK
 PASSES = K // K_PASS
+QUADRANTS = 4
+PAIR = 2
 HALF = S // 2
-V_COLS = 144
+VECTOR_COLUMNS = 144
+GPSIMD_TILES = 3
 
 
 def tile_picked_ykal_mean_po_kernel(
@@ -28,188 +31,181 @@ def tile_picked_ykal_mean_po_kernel(
 ):
     nc = tc.nc
     with ExitStack() as ctx:
-        keep = ctx.enter_context(tc.tile_pool(name="keep", bufs=1))
+        sbuf = ctx.enter_context(tc.tile_pool(name="keep", bufs=1))
         psum = ctx.enter_context(tc.psum_pool(name="psum", bufs=1))
 
         def sb(name, shape, dtype):
-            return keep.tile(shape, dtype, name=name, align_bytes=64)
+            return sbuf.tile(shape, dtype, name=name, align_bytes=64)
 
-        offs_t = keep.tile([P, S // 16], U16, name="offs_t")
-        track_t = keep.tile([P, S // 16], U16, name="track_t")
+        offs_list = sbuf.tile([P, S // 16], U16, name="offs_t")
+        track_list = sbuf.tile([P, S // 16], U16, name="track_t")
+        nc.sync.dma_start(track_list[:], track)
 
-        xs = sb("xs", [P, T], U8)
-        nc.vector.memset(xs[:].bitcast(I32), 0)
+        x_scale_table = sb("xs", [P, T], U8)
+        nc.vector.memset(x_scale_table[:].bitcast(I32), 0)
 
+        def load_words(g):
+            table = sb("xw%d" % g, [P, T], U32)
+            nc.sync.dma_start(table[:].bitcast(I32), x_words[g].rearrange("p n t -> p (n t)").bitcast(I32))
+            return table
 
-        def load_x(g):
-            t_ = sb("xw%d" % g, [P, T], U32)
-            nc.sync.dma_start(t_[:].bitcast(I32), x_words[g].rearrange("p n t -> p (n t)").bitcast(I32))
-            return t_
+        def load_weight(w, name, g):
+            raw = sb(name, [P, PACK, N], F32)
+            nc.sync.dma_start(raw[:], w[g * K_PASS : (g + 1) * K_PASS, :].rearrange("(p j) n -> p j n", j=PACK))
+            return raw
 
-        def load_w(w, name, g):
-            t_ = sb(name, [P, PACK, N], F32)
-            nc.sync.dma_start(t_[:], w[g * K_PASS : (g + 1) * K_PASS, :].rearrange("(p j) n -> p j n", j=PACK))
-            return t_
+        def load_row_tile(src, name, t):
+            table = sb(name, [P, U], F32)
+            nc.sync.dma_start(table[:], src.rearrange("(p t) u -> p t u", t=PACK)[:, t, :])
+            return table
 
-        def load_rows(src, name, t):
-            t_ = sb(name, [P, U], F32)
-            nc.sync.dma_start(t_[:], src.rearrange("(p t) u -> p t u", t=PACK)[:, t, :])
-            return t_
-
-        def load_pair(t):
-            t_ = sb("var%d" % t, [P, 2, U], F32)
-            nc.sync.dma_start(t_[:], var.rearrange("(p t) u -> p t u", t=PACK)[:, t : t + 2, :])
-            return [t_[:, 0, :], t_[:, 1, :]]
-
-        nc.sync.dma_start(offs_t[:], offs)
-        xw0 = load_x(0)
-        nc.sync.dma_start(track_t[:], track)
-        for q in range(4):
-            nc.sync.dma_start(xs[32 * q : 32 * q + 8, :].bitcast(I32), x_scales[:, 4 * q : 4 * q + 4, :].bitcast(I32))
-        var_t = load_pair(0) + load_pair(2)
-        w2a = load_w(w2, "w2a", 0)
-        xw1 = load_x(1)
-        w2b = load_w(w2, "w2b", 1)
-        mean_t = [load_rows(mean, "mean0", 0)]
-        w1a = load_w(w1, "w1a", 0)
-        mean_t.extend([load_rows(mean, "mean%d" % t, t) for t in range(1, 3)])
-        w1b = load_w(w1, "w1b", 1)
-        mean_t.append(load_rows(mean, "mean3", 3))
-
-        lnva = []
-
-        def var_part(t):
-            va = sb("va%d" % t, [P, S], F32)
-            nc.vector.tensor_copy(va[:], var_t[t].indirect(track_t[:]))
-            l_ = sb("ln%d" % t, [P, S], F32)
-            nc.scalar.activation(l_[:], va[:], ACT.Ln)
-            lnva.append(l_)
-            return va
-
-        xg = []
-
-        def x_part(g, xw):
-            t_ = sb("xg%d" % g, [P, S], U32)
-            nc.vector.tensor_copy(t_[:], xw[:].indirect(offs_t[:]))
-            xg.append(t_)
-
-        x_part(0, xw0)
-        xsg = sb("xsg", [P, S], U8)
-        nc.vector.tensor_copy(xsg[:], xs[:].indirect(offs_t[:]))
-        for t in range(4):
-            var_part(t)
-
-        def cast(eng, dst, raw, m0, m1, t0, t1):
-            o = dst[:, :, m0:m1, :].rearrange("p t m j -> p m j t")
-            i = raw[:].rearrange("p j (m t) -> p m j t", t=PACK)[:, m0:m1, :, t0:t1]
-            if eng == "v":
-                nc.vector.tensor_copy(o, i)
-            else:
-                nc.scalar.copy(o, i)
-
-        def quant_tiles(name, src, n_tiles):
-            c_ = sb("%sc" % name, [P, n_tiles * P], U32)
-            s_ = sb("%ss" % name, [P, n_tiles * P], U8)
-            nc.vector.quantize_mx(out=c_[:].bitcast(FP8X4), scales=s_[:], in_=src.rearrange("p t m j -> p (t m j)"))
-            return [(c_[:, t * P : (t + 1) * P], s_[:, t * P : (t + 1) * P]) for t in range(n_tiles)]
-
-        def quant_pairs(name, raw, engines):
-            staged = []
-            for t0, eng in zip((0, 2), engines):
-                wb = sb("%sb%d" % (name, t0), [P, 2, P, PACK], BF16)
-                cast(eng, wb, raw, 0, P, t0, t0 + 2)
-                staged.append(wb)
-            return quant_tiles(name + "0", staged[0][:], 2) + quant_tiles(name + "1", staged[1][:], 2)
-
-        def mm(acc, q, g):
-            nc.tensor.matmul_mx(
-                out=acc[:],
-                lhsT=q[0].bitcast(FP8X4),
-                lhsT_scale=q[1],
-                rhs=xg[g][:].bitcast(FP8X4),
-                rhs_scale=xsg[4 * g : P, :],
-                start=(g == 0),
-                stop=(g == PASSES - 1),
+        var_tables = [load_row_tile(var, "var%d" % t, t) for t in range(PAIR)]
+        nc.sync.dma_start(offs_list[:], offs)
+        for quad in range(QUADRANTS):
+            nc.sync.dma_start(
+                x_scale_table[32 * quad : 32 * quad + 4 * PASSES, :].bitcast(I32),
+                x_scales[:, 4 * quad : 4 * quad + 4, :].bitcast(I32),
             )
+        var_tables.extend([load_row_tile(var, "var%d" % t, t) for t in range(PAIR, PACK)])
+        word_table_0 = load_words(0)
+        w2_raw_0 = load_weight(w2, "w2a", 0)
+        word_table_1 = load_words(1)
+        w2_raw_1 = load_weight(w2, "w2b", 1)
+        w1_raw_0 = load_weight(w1, "w1a", 0)
+        mean_tables = [load_row_tile(mean, "mean%d" % t, t) for t in range(PACK - 1)]
+        w1_raw_1 = load_weight(w1, "w1b", 1)
+        mean_tables.append(load_row_tile(mean, "mean%d" % (PACK - 1), PACK - 1))
 
-        zb = [psum.tile([P, S], F32, name="z%d" % t) for t in range(4)]
-        yb = [psum.tile([P, S], F32, name="y%d" % t) for t in range(4)]
+        log_var = []
+        for t in range(PACK):
+            picked_var = sb("va%d" % t, [P, S], F32)
+            nc.vector.tensor_copy(picked_var[:], var_tables[t][:].indirect(track_list[:]))
+            log_tile = sb("ln%d" % t, [P, S], F32)
+            nc.scalar.activation(log_tile[:], picked_var[:], ACT.Ln)
+            log_var.append(log_tile)
+        table_preload = sb("preload", [P, 1], F32)
+        nc.scalar.activation(table_preload[:], log_var[PACK - 1][:, 0:1], ACT.Sigmoid)
 
-        q = quant_pairs("w2a", w2a, "vs")
-        for t in range(4):
-            mm(zb[t], q[t], 0)
-        x_part(1, xw1)
-        q = quant_pairs("w2b", w2b, "vs")
-        for t in range(4):
-            mm(zb[t], q[t], 1)
-        mu0 = sb("mu0", [P, S], F32)
-        nc.vector.tensor_copy(mu0[:], mean_t[0][:].indirect(track_t[:]))
-        keepw = []
-        w1a_b = sb("w1ab", [P, PACK, P, PACK], BF16)
-        for t in range(4):
-            a_ = sb("a%d" % t, [P, S], F32)
-            nc.vector.tensor_tensor(a_[:], zb[t][:], lnva[t][:], ALU.subtract)
-            if t == 2:
-                cast("s", w1a_b, w1a, 0, P, 0, 4)
-                h_ = keep.tile([P, S], F32, name="h2", tag="w1a", align_bytes=64)
-            else:
-                h_ = sb("h%d" % t, [P, S], F32)
-            nc.scalar.activation(h_[:], a_[:], ACT.Sigmoid)
-            keepw.append(h_)
-        rest = []
+        x_codes = []
 
-        def mean_part(t):
-            r_ = sb("r%d" % t, [P, S], F32)
-            nc.vector.tensor_tensor(r_[:], mu0[:] if t == 0 else mean_t[t][:].indirect(track_t[:]), keepw[t][:], ALU.mult)
-            rest.append(r_)
+        def gather_words(g, table):
+            picked = sb("xg%d" % g, [P, S], U32)
+            nc.vector.tensor_copy(picked[:], table[:].indirect(offs_list[:]))
+            x_codes.append(picked)
 
-        for t in range(2):
-            mean_part(t)
-        q = quant_tiles("w1a", w1a_b[:], 4)
-        for t in range(4):
-            mm(yb[t], q[t], 0)
-        mean_part(2)
-        q = quant_pairs("w1b", w1b, "ss")
-        for t in range(4):
-            mm(yb[t], q[t], 1)
-        mean_part(3)
+        gather_words(0, word_table_0)
+        x_scale_bytes = sb("xsg", [P, S], U8)
+        nc.vector.tensor_copy(x_scale_bytes[:], x_scale_table[:].indirect(offs_list[:]))
+
+        def round_pair(name, raw, t0, copy):
+            rounded = sb("%sb%d" % (name, t0), [P, PAIR, P, PACK], BF16)
+            copy(
+                rounded[:].rearrange("p t c j -> p c j t"),
+                raw[:].rearrange("p j (c t) -> p c j t", t=PACK)[:, :, :, t0 : t0 + PAIR],
+            )
+            return rounded
+
+        def quantise_pair(name, rounded):
+            codes = sb("%sc" % name, [P, PAIR * P], U32)
+            scales = sb("%ss" % name, [P, PAIR * P], U8)
+            nc.vector.quantize_mx(
+                out=codes[:].bitcast(FP8X4), scales=scales[:], in_=rounded[:].rearrange("p t c j -> p (t c j)")
+            )
+            return [(codes[:, t * P : (t + 1) * P], scales[:, t * P : (t + 1) * P]) for t in range(PAIR)]
+
+        def quantise_pass(name, raw, first_copy, second_copy):
+            first = round_pair(name, raw, 0, first_copy)
+            second = round_pair(name, raw, PAIR, second_copy)
+            return quantise_pair(name + "0", first) + quantise_pair(name + "1", second)
+
+        def multiply_pass(banks, weights, g):
+            for bank, (codes, scales) in zip(banks, weights):
+                nc.tensor.matmul_mx(
+                    out=bank[:],
+                    lhsT=codes.bitcast(FP8X4),
+                    lhsT_scale=scales,
+                    rhs=x_codes[g][:].bitcast(FP8X4),
+                    rhs_scale=x_scale_bytes[4 * g : P, :],
+                    start=(g == 0),
+                    stop=(g == PASSES - 1),
+                )
+
+        z_banks = [psum.tile([P, S], F32, name="z%d" % t) for t in range(PACK)]
+        y_banks = [psum.tile([P, S], F32, name="y%d" % t) for t in range(PACK)]
+
+        multiply_pass(z_banks, quantise_pass("w2a", w2_raw_0, nc.vector.tensor_copy, nc.scalar.copy), 0)
+        gather_words(1, word_table_1)
+        multiply_pass(z_banks, quantise_pass("w2b", w2_raw_1, nc.vector.tensor_copy, nc.scalar.copy), 1)
+
+        w1_first_pair = round_pair("w1a", w1_raw_0, 0, nc.scalar.copy)
+        keep = []
+        for t in range(PACK):
+            logit = sb("a%d" % t, [P, S], F32)
+            nc.vector.tensor_tensor(logit[:], z_banks[t][:], log_var[t][:], ALU.subtract)
+            keep_tile = sb("h%d" % t, [P, S], F32)
+            nc.scalar.activation(keep_tile[:], logit[:], ACT.Sigmoid)
+            keep.append(keep_tile)
+        w1_pass_0 = quantise_pair("w1a0", w1_first_pair)
+
+        kept_mean = []
+
+        def gather_kept_mean(t):
+            product = sb("r%d" % t, [P, S], F32)
+            nc.vector.tensor_tensor(product[:], mean_tables[t][:].indirect(track_list[:]), keep[t][:], ALU.mult)
+            kept_mean.append(product)
+
+        for t in range(PACK - 1):
+            gather_kept_mean(t)
+        w1_pass_0 = w1_pass_0 + quantise_pair("w1a1", round_pair("w1a", w1_raw_0, PAIR, nc.scalar.copy))
+        multiply_pass(y_banks, w1_pass_0, 0)
+        multiply_pass(y_banks, quantise_pass("w1b", w1_raw_1, nc.scalar.copy, nc.scalar.copy), 1)
+        gather_kept_mean(PACK - 1)
 
         out_rows = out_0.rearrange("(p t) s -> p t s", t=PACK)
-        words = out_1[0].rearrange("p c r -> p (c r)").bitcast(I32)
-        oc = sb("oc", [P, S], U32)
-        osc = sb("osc", [P, S], U8)
-        staged = []
-        prods = {}
-        for pair in range(2):
-            for h in range(2):
-                cols = slice(h * HALF, (h + 1) * HALF)
-                for t in (2 * pair, 2 * pair + 1):
-                    p_ = sb("p%d%d" % (h, t), [P, HALF], F32)
-                    nc.vector.scalar_tensor_tensor(p_[:], keepw[t][:, cols], 1.0, yb[t][:, cols], ALU.subtract, ALU.mult)
-                    prods[(h, t)] = p_
-        for h in range(2):
-            cols = slice(h * HALF, (h + 1) * HALF)
-            res = sb("res%d" % h, [P, PACK, HALF], F32)
-            for t in range(4):
-                eng = nc.gpsimd if h == 0 and t < 3 else nc.vector
-                eng.tensor_tensor(res[:, t, :], rest[t][:, cols], prods[(h, t)][:], ALU.subtract)
-                if t % 2 == 1:
-                    nc.sync.dma_start(out_rows[:, t - 1 : t + 1, cols], res[:, t - 1 : t + 1, :])
-            rb = sb("rb%d" % h, [P, HALF, PACK], BF16)
-            o = rb[:].rearrange("p (c i) t -> p c t i", i=4)
-            i = res[:].rearrange("p t (c i) -> p c t i", i=4)
+        out_words = out_1[0].rearrange("p c r -> p (c r)").bitcast(I32)
+        result_codes = sb("oc", [P, S], U32)
+        result_scales = sb("osc", [P, S], U8)
+        halves = [slice(h * HALF, (h + 1) * HALF) for h in range(2)]
+
+        weighted_y = {}
+        for t0 in range(0, PACK, PAIR):
+            for h, cols in enumerate(halves):
+                for t in range(t0, t0 + PAIR):
+                    product = sb("p%d%d" % (h, t), [P, HALF], F32)
+                    nc.vector.scalar_tensor_tensor(
+                        product[:], keep[t][:, cols], 1.0, y_banks[t][:, cols], ALU.subtract, ALU.mult
+                    )
+                    weighted_y[(h, t)] = product
+
+        rounded_halves = []
+        for h, cols in enumerate(halves):
+            result = sb("res%d" % h, [P, PACK, HALF], F32)
+            for t in range(PACK):
+                engine = nc.gpsimd if h == 0 and t < GPSIMD_TILES else nc.vector
+                engine.tensor_tensor(result[:, t, :], kept_mean[t][:, cols], weighted_y[(h, t)][:], ALU.subtract)
+                if t % PAIR == PAIR - 1:
+                    rows = slice(t + 1 - PAIR, t + 1)
+                    nc.sync.dma_start(out_rows[:, rows, cols], result[:, rows, :])
+            rounded = sb("rb%d" % h, [P, HALF, PACK], BF16)
+            dst = rounded[:].rearrange("p (c i) t -> p c t i", i=4)
+            src = result[:].rearrange("p t (c i) -> p c t i", i=4)
             if h == 0:
-                nc.scalar.copy(o, i)
+                nc.scalar.copy(dst, src)
             else:
-                nc.vector.tensor_copy(o[:, : V_COLS // 4], i[:, : V_COLS // 4])
-                nc.scalar.copy(o[:, V_COLS // 4 :], i[:, V_COLS // 4 :])
-            staged.append(rb)
-        for h in range(2):
-            cols = slice(h * HALF, (h + 1) * HALF)
-            nc.vector.quantize_mx(out=oc[:, cols].bitcast(FP8X4), scales=osc[:, cols], in_=staged[h][:].rearrange("p c t -> p (c t)"))
-            if h == 0:
-                nc.sync.dma_start(words[:, cols], oc[:, cols].bitcast(I32))
-        nc.sync.dma_start(words[:, HALF:], oc[:, HALF:].bitcast(I32))
-        for qd in range(4):
-            eng = nc.sync if qd == 3 else nc.scalar
-            eng.dma_start(out_2[0, 4 * qd : 4 * qd + 4, :].bitcast(I32), osc[32 * qd : 32 * qd + 4, :].bitcast(I32))
+                nc.vector.tensor_copy(dst[:, : VECTOR_COLUMNS // 4], src[:, : VECTOR_COLUMNS // 4])
+                nc.scalar.copy(dst[:, VECTOR_COLUMNS // 4 :], src[:, VECTOR_COLUMNS // 4 :])
+            rounded_halves.append(rounded)
+
+        for rounded, cols in zip(rounded_halves, halves):
+            nc.vector.quantize_mx(
+                out=result_codes[:, cols].bitcast(FP8X4),
+                scales=result_scales[:, cols],
+                in_=rounded[:].rearrange("p c t -> p (c t)"),
+            )
+            nc.sync.dma_start(out_words[:, cols], result_codes[:, cols].bitcast(I32))
+        for quad in range(QUADRANTS):
+            engine = nc.sync if quad == QUADRANTS - 1 else nc.scalar
+            engine.dma_start(
+                out_2[0, 4 * quad : 4 * quad + 4, :].bitcast(I32),
+                result_scales[32 * quad : 32 * quad + 4, :].bitcast(I32),
+            )

@@ -83,8 +83,6 @@ def tile_picked_ykal_mean_po_kernel(
             log_tile = sb("ln%d" % t, [P, S], F32)
             nc.scalar.activation(log_tile[:], picked_var[:], ACT.Ln)
             log_var.append(log_tile)
-        table_preload = sb("preload", [P, 1], F32)
-        nc.scalar.activation(table_preload[:], log_var[PACK - 1][:, 0:1], ACT.Sigmoid)
 
         x_codes = []
 

@@ -39,7 +39,6 @@ def tile_picked_ykal_mean_po_kernel(
 
         offs_list = sbuf.tile([P, S // 16], U16, name="offs_t")
         track_list = sbuf.tile([P, S // 16], U16, name="track_t")
-        nc.sync.dma_start(track_list[:], track)
 
         x_scale_table = sb("xs", [P, T], U8)
         nc.vector.memset(x_scale_table[:].bitcast(I32), 0)
@@ -59,30 +58,29 @@ def tile_picked_ykal_mean_po_kernel(
             nc.sync.dma_start(table[:], src.rearrange("(p t) u -> p t u", t=PACK)[:, t, :])
             return table
 
-        var_tables = [load_row_tile(var, "var%d" % t, t) for t in range(PAIR)]
+        var_tables = []
+        mean_tables = []
         nc.sync.dma_start(offs_list[:], offs)
+        word_table_0 = load_words(0)
         for quad in range(QUADRANTS):
             nc.sync.dma_start(
                 x_scale_table[32 * quad : 32 * quad + 4 * PASSES, :].bitcast(I32),
                 x_scales[:, 4 * quad : 4 * quad + 4, :].bitcast(I32),
             )
-        var_tables.extend([load_row_tile(var, "var%d" % t, t) for t in range(PAIR, PACK)])
-        word_table_0 = load_words(0)
+        nc.sync.dma_start(track_list[:], track)
         w2_raw_0 = load_weight(w2, "w2a", 0)
         word_table_1 = load_words(1)
         w2_raw_1 = load_weight(w2, "w2b", 1)
+        var_tables.append(load_row_tile(var, "var0", 0))
+        var_tables.append(load_row_tile(var, "var1", 1))
+        var_tables.append(load_row_tile(var, "var2", 2))
+        var_tables.append(load_row_tile(var, "var3", 3))
         w1_raw_0 = load_weight(w1, "w1a", 0)
-        mean_tables = [load_row_tile(mean, "mean%d" % t, t) for t in range(PACK - 1)]
+        mean_tables.append(load_row_tile(mean, "mean0", 0))
+        mean_tables.append(load_row_tile(mean, "mean1", 1))
         w1_raw_1 = load_weight(w1, "w1b", 1)
-        mean_tables.append(load_row_tile(mean, "mean%d" % (PACK - 1), PACK - 1))
-
-        log_var = []
-        for t in range(PACK):
-            picked_var = sb("va%d" % t, [P, S], F32)
-            nc.vector.tensor_copy(picked_var[:], var_tables[t][:].indirect(track_list[:]))
-            log_tile = sb("ln%d" % t, [P, S], F32)
-            nc.scalar.activation(log_tile[:], picked_var[:], ACT.Ln)
-            log_var.append(log_tile)
+        mean_tables.append(load_row_tile(mean, "mean2", 2))
+        mean_tables.append(load_row_tile(mean, "mean3", 3))
 
         x_codes = []
 
@@ -95,10 +93,13 @@ def tile_picked_ykal_mean_po_kernel(
         x_scale_bytes = sb("xsg", [P, S], U8)
         nc.vector.tensor_copy(x_scale_bytes[:], x_scale_table[:].indirect(offs_list[:]))
 
-        def round_pair(name, raw, t0, copy):
-            rounded = sb("%sb%d" % (name, t0), [P, PAIR, P, PACK], BF16)
+        def round_pair(name, raw, t0, copy, reused=None):
+            if reused is None:
+                rounded = sb("%sb%d" % (name, t0), [P, PAIR * P * PACK], BF16)[:]
+            else:
+                rounded = reused[:].bitcast(BF16)
             copy(
-                rounded[:].rearrange("p t c j -> p c j t"),
+                rounded.rearrange("p (t c j) -> p c j t", t=PAIR, j=PACK),
                 raw[:].rearrange("p j (c t) -> p c j t", t=PACK)[:, :, :, t0 : t0 + PAIR],
             )
             return rounded
@@ -107,7 +108,7 @@ def tile_picked_ykal_mean_po_kernel(
             codes = sb("%sc" % name, [P, PAIR * P], U32)
             scales = sb("%ss" % name, [P, PAIR * P], U8)
             nc.vector.quantize_mx(
-                out=codes[:].bitcast(FP8X4), scales=scales[:], in_=rounded[:].rearrange("p t c j -> p (t c j)")
+                out=codes[:].bitcast(FP8X4), scales=scales[:], in_=rounded
             )
             return [(codes[:, t * P : (t + 1) * P], scales[:, t * P : (t + 1) * P]) for t in range(PAIR)]
 
@@ -135,64 +136,102 @@ def tile_picked_ykal_mean_po_kernel(
         gather_words(1, word_table_1)
         multiply_pass(z_banks, quantise_pass("w2b", w2_raw_1, nc.vector.tensor_copy, nc.scalar.copy), 1)
 
-        w1_first_pair = round_pair("w1a", w1_raw_0, 0, nc.scalar.copy)
-        keep = []
+        decay = [sb("e%d" % t, [P, S], F32) for t in range(PACK)]
+        keep = [sb("h%d" % t, [P, S], F32) for t in range(PACK)]
         for t in range(PACK):
-            logit = sb("a%d" % t, [P, S], F32)
-            nc.vector.tensor_tensor(logit[:], z_banks[t][:], log_var[t][:], ALU.subtract)
-            keep_tile = sb("h%d" % t, [P, S], F32)
-            nc.scalar.activation(keep_tile[:], logit[:], ACT.Sigmoid)
-            keep.append(keep_tile)
-        w1_pass_0 = quantise_pair("w1a0", w1_first_pair)
+            nc.scalar.activation(decay[t][:], z_banks[t][:], ACT.Exp, scale=-1.0)
+        for t in range(PACK):
+            nc.vector.tensor_tensor(keep[t][:], var_tables[t][:].indirect(track_list[:]), decay[t][:], ALU.mult)
 
-        kept_mean = []
+        def finish_keep(t):
+            nc.scalar.activation(decay[t][:], keep[t][:], ACT.Abs_reciprocal_sqrt, bias=1.0)
+            nc.scalar.activation(keep[t][:], decay[t][:], ACT.Square)
 
-        def gather_kept_mean(t):
-            product = sb("r%d" % t, [P, S], F32)
-            nc.vector.tensor_tensor(product[:], mean_tables[t][:].indirect(track_list[:]), keep[t][:], ALU.mult)
-            kept_mean.append(product)
+        kept_mean = [sb("r%d" % t, [P, S], F32) for t in range(PACK - 1)]
 
-        for t in range(PACK - 1):
-            gather_kept_mean(t)
-        w1_pass_0 = w1_pass_0 + quantise_pair("w1a1", round_pair("w1a", w1_raw_0, PAIR, nc.scalar.copy))
-        multiply_pass(y_banks, w1_pass_0, 0)
-        multiply_pass(y_banks, quantise_pass("w1b", w1_raw_1, nc.scalar.copy, nc.scalar.copy), 1)
-        gather_kept_mean(PACK - 1)
+        def gather_kept_mean(t, first, last):
+            nc.vector.tensor_tensor(
+                kept_mean[t][:, first:last],
+                mean_tables[t][:].indirect(track_list[:, first // 16 : last // 16]),
+                keep[t][:, first:last],
+                ALU.mult,
+            )
+
+        w1a_first = round_pair("w1a", w1_raw_0, 0, nc.vector.tensor_copy)
+        finish_keep(0)
+        finish_keep(1)
+        gather_kept_mean(0, 0, S)
+        w1a_second = round_pair("w1a", w1_raw_0, PAIR, nc.scalar.copy, decay[1])
+        multiply_pass(y_banks[:PAIR], quantise_pair("w1a0", w1a_first), 0)
+        gather_kept_mean(1, 0, S)
+        multiply_pass(y_banks[PAIR:], quantise_pair("w1a1", w1a_second), 0)
+        finish_keep(2)
+        finish_keep(3)
+        w1b_first = round_pair("w1b", w1_raw_1, 0, nc.vector.tensor_copy)
+        w1b_second = round_pair("w1b", w1_raw_1, PAIR, nc.scalar.copy)
+        multiply_pass(y_banks[:PAIR], quantise_pair("w1b0", w1b_first), 1)
+        gather_kept_mean(2, 0, S)
+        multiply_pass(y_banks[PAIR:], quantise_pair("w1b1", w1b_second), 1)
 
         out_rows = out_0.rearrange("(p t) s -> p t s", t=PACK)
         out_words = out_1[0].rearrange("p c r -> p (c r)").bitcast(I32)
         result_codes = sb("oc", [P, S], U32)
         result_scales = sb("osc", [P, S], U8)
         halves = [slice(h * HALF, (h + 1) * HALF) for h in range(2)]
+        results = [sb("res%d" % h, [P, PACK, HALF], F32) for h in range(2)]
+        rounded_halves = [sb("rb%d" % h, [P, HALF, PACK], BF16) for h in range(2)]
+        weighted_y = [sb("p%d" % t, [P, S], F32) for t in range(PACK)]
 
-        weighted_y = {}
-        for t0 in range(0, PACK, PAIR):
-            for h, cols in enumerate(halves):
-                for t in range(t0, t0 + PAIR):
-                    product = sb("p%d%d" % (h, t), [P, HALF], F32)
-                    nc.vector.scalar_tensor_tensor(
-                        product[:], keep[t][:, cols], 1.0, y_banks[t][:, cols], ALU.subtract, ALU.mult
-                    )
-                    weighted_y[(h, t)] = product
+        def weigh_y(t, h):
+            cols = halves[h]
+            nc.vector.scalar_tensor_tensor(
+                weighted_y[t][:, cols], keep[t][:, cols], 1.0, y_banks[t][:, cols], ALU.subtract, ALU.mult
+            )
 
-        rounded_halves = []
-        for h, cols in enumerate(halves):
-            result = sb("res%d" % h, [P, PACK, HALF], F32)
-            for t in range(PACK):
-                engine = nc.gpsimd if h == 0 and t < GPSIMD_TILES else nc.vector
-                engine.tensor_tensor(result[:, t, :], kept_mean[t][:, cols], weighted_y[(h, t)][:], ALU.subtract)
-                if t % PAIR == PAIR - 1:
-                    rows = slice(t + 1 - PAIR, t + 1)
-                    nc.sync.dma_start(out_rows[:, rows, cols], result[:, rows, :])
-            rounded = sb("rb%d" % h, [P, HALF, PACK], BF16)
-            dst = rounded[:].rearrange("p (c i) t -> p c t i", i=4)
-            src = result[:].rearrange("p t (c i) -> p c t i", i=4)
-            if h == 0:
-                nc.scalar.copy(dst, src)
-            else:
-                nc.vector.tensor_copy(dst[:, : VECTOR_COLUMNS // 4], src[:, : VECTOR_COLUMNS // 4])
-                nc.scalar.copy(dst[:, VECTOR_COLUMNS // 4 :], src[:, VECTOR_COLUMNS // 4 :])
-            rounded_halves.append(rounded)
+        def difference(engine, t, h, kept):
+            engine.tensor_tensor(results[h][:, t, :], kept, weighted_y[t][:, halves[h]], ALU.subtract)
+
+        def store_pair(t0, h):
+            rows = slice(t0, t0 + PAIR)
+            nc.sync.dma_start(out_rows[:, rows, halves[h]], results[h][:, rows, :])
+
+        def round_columns(copy, h, first, last):
+            dst = rounded_halves[h][:].rearrange("p (c i) t -> p c t i", i=4)
+            src = results[h][:].rearrange("p t (c i) -> p c t i", i=4)
+            copy(dst[:, first // 4 : last // 4], src[:, first // 4 : last // 4])
+
+        def gather_last(out, h):
+            cols = halves[h]
+            nc.vector.tensor_tensor(
+                out, mean_tables[3][:].indirect(track_list[:, cols.start // 16 : cols.stop // 16]), keep[3][:, cols], ALU.mult
+            )
+
+        last_first_half = sb("r3", [P, HALF], F32)[:]
+        gather_last(last_first_half, 0)
+        weigh_y(0, 0)
+        weigh_y(1, 0)
+        difference(nc.gpsimd, 0, 0, kept_mean[0][:, halves[0]])
+        weigh_y(0, 1)
+        weigh_y(1, 1)
+        difference(nc.gpsimd, 1, 0, kept_mean[1][:, halves[0]])
+        store_pair(0, 0)
+        weigh_y(2, 0)
+        weigh_y(3, 0)
+        difference(nc.vector, 2, 0, kept_mean[2][:, halves[0]])
+        difference(nc.vector, 3, 0, last_first_half)
+        store_pair(2, 0)
+        round_columns(nc.scalar.copy, 0, 0, HALF)
+        weigh_y(2, 1)
+        weigh_y(3, 1)
+        difference(nc.gpsimd, 0, 1, kept_mean[0][:, halves[1]])
+        gather_last(last_first_half, 1)
+        difference(nc.vector, 1, 1, kept_mean[1][:, halves[1]])
+        store_pair(0, 1)
+        difference(nc.vector, 2, 1, kept_mean[2][:, halves[1]])
+        difference(nc.vector, 3, 1, last_first_half)
+        store_pair(2, 1)
+        round_columns(nc.vector.tensor_copy, 1, 0, VECTOR_COLUMNS)
+        round_columns(nc.scalar.copy, 1, VECTOR_COLUMNS, HALF)
 
         for rounded, cols in zip(rounded_halves, halves):
             nc.vector.quantize_mx(

@@ -69,8 +69,8 @@ def tile_picked_ykal_mean_po_kernel(
             )
         nc.sync.dma_start(track_list[:], track)
         w2_raw_0 = load_weight(w2, "w2a", 0)
-        word_table_1 = load_words(1)
         w2_raw_1 = load_weight(w2, "w2b", 1)
+        word_table_1 = load_words(1)
         var_tables.append(load_row_tile(var, "var0", 0))
         var_tables.append(load_row_tile(var, "var1", 1))
         var_tables.append(load_row_tile(var, "var2", 2))
@@ -82,14 +82,12 @@ def tile_picked_ykal_mean_po_kernel(
         mean_tables.append(load_row_tile(mean, "mean2", 2))
         mean_tables.append(load_row_tile(mean, "mean3", 3))
 
-        x_codes = []
+        x_codes = [sb("xg%d" % g, [P, S], U32) for g in range(PASSES)]
 
-        def gather_words(g, table):
-            picked = sb("xg%d" % g, [P, S], U32)
-            nc.vector.tensor_copy(picked[:], table[:].indirect(offs_list[:]))
-            x_codes.append(picked)
+        def gather_words(g, table, first, last):
+            nc.vector.tensor_copy(x_codes[g][:, first:last], table[:].indirect(offs_list[:, first // 16 : last // 16]))
 
-        gather_words(0, word_table_0)
+        gather_words(0, word_table_0, 0, S)
         x_scale_bytes = sb("xsg", [P, S], U8)
         nc.vector.tensor_copy(x_scale_bytes[:], x_scale_table[:].indirect(offs_list[:]))
 
@@ -117,37 +115,65 @@ def tile_picked_ykal_mean_po_kernel(
             second = round_pair(name, raw, PAIR, second_copy)
             return quantise_pair(name + "0", first) + quantise_pair(name + "1", second)
 
+        def multiply(bank, weights, g, first=0, last=S):
+            codes, scales = weights
+            nc.tensor.matmul_mx(
+                out=bank,
+                lhsT=codes.bitcast(FP8X4),
+                lhsT_scale=scales,
+                rhs=x_codes[g][:, first:last].bitcast(FP8X4),
+                rhs_scale=x_scale_bytes[4 * g : P, first:last],
+                start=(g == 0),
+                stop=(g == PASSES - 1),
+            )
+
         def multiply_pass(banks, weights, g):
-            for bank, (codes, scales) in zip(banks, weights):
-                nc.tensor.matmul_mx(
-                    out=bank[:],
-                    lhsT=codes.bitcast(FP8X4),
-                    lhsT_scale=scales,
-                    rhs=x_codes[g][:].bitcast(FP8X4),
-                    rhs_scale=x_scale_bytes[4 * g : P, :],
-                    start=(g == 0),
-                    stop=(g == PASSES - 1),
-                )
+            for bank, tile_weights in zip(banks, weights):
+                multiply(bank[:], tile_weights, g)
 
-        z_banks = [psum.tile([P, S], F32, name="z%d" % t) for t in range(PACK)]
-        y_banks = [psum.tile([P, S], F32, name="y%d" % t) for t in range(PACK)]
+        z_halves = [psum.tile([P, HALF], F32, name="zh%d" % h, tag="bank%d" % h) for h in range(2)]
+        z_banks = [psum.tile([P, S], F32, name="z%d" % t, tag="bank%d" % (t + 1)) for t in range(1, PACK)]
 
-        multiply_pass(z_banks, quantise_pass("w2a", w2_raw_0, nc.vector.tensor_copy, nc.scalar.copy), 0)
-        gather_words(1, word_table_1)
-        multiply_pass(z_banks, quantise_pass("w2b", w2_raw_1, nc.vector.tensor_copy, nc.scalar.copy), 1)
+        w2_pass_0 = quantise_pass("w2a", w2_raw_0, nc.vector.tensor_copy, nc.scalar.copy)
+        for h in range(2):
+            multiply(z_halves[h][:], w2_pass_0[0], 0, h * HALF, (h + 1) * HALF)
+        multiply_pass(z_banks, w2_pass_0[1:], 0)
+        w2b_first = round_pair("w2b", w2_raw_1, 0, nc.vector.tensor_copy)
+        w2b_second = round_pair("w2b", w2_raw_1, PAIR, nc.scalar.copy)
+        w2_pass_1 = quantise_pair("w2b0", w2b_first)
+        gather_words(1, word_table_1, 0, HALF)
+        multiply(z_halves[0][:], w2_pass_1[0], 1, 0, HALF)
+        gather_words(1, word_table_1, HALF, S)
+        multiply(z_halves[1][:], w2_pass_1[0], 1, HALF, S)
+        w2_pass_1 = w2_pass_1 + quantise_pair("w2b1", w2b_second)
+        multiply_pass(z_banks, w2_pass_1[1:], 1)
 
         decay = [sb("e%d" % t, [P, S], F32) for t in range(PACK)]
         keep = [sb("h%d" % t, [P, S], F32) for t in range(PACK)]
-        for t in range(PACK):
-            nc.scalar.activation(decay[t][:], z_banks[t][:], ACT.Exp, scale=-1.0)
-        for t in range(PACK):
-            nc.vector.tensor_tensor(keep[t][:], var_tables[t][:].indirect(track_list[:]), decay[t][:], ALU.mult)
+        for h in range(2):
+            nc.scalar.activation(decay[0][:, h * HALF : (h + 1) * HALF], z_halves[h][:], ACT.Exp, scale=-1.0)
+        for t in range(1, PACK):
+            nc.scalar.activation(decay[t][:], z_banks[t - 1][:], ACT.Exp, scale=-1.0)
+        y_banks = [psum.tile([P, S], F32, name="y%d" % t, tag="bank%d" % ((t + PACK + 1) % (2 * PACK))) for t in range(PACK)]
+
+        def gather_ratio(t, first, last):
+            nc.vector.tensor_tensor(
+                keep[t][:, first:last],
+                var_tables[t][:].indirect(track_list[:, first // 16 : last // 16]),
+                decay[t][:, first:last],
+                ALU.mult,
+            )
+
+        gather_ratio(0, 0, HALF)
+        gather_ratio(0, HALF, S)
+        for t in range(1, PACK):
+            gather_ratio(t, 0, S)
 
         def finish_keep(t):
             nc.scalar.activation(decay[t][:], keep[t][:], ACT.Abs_reciprocal_sqrt, bias=1.0)
             nc.scalar.activation(keep[t][:], decay[t][:], ACT.Square)
 
-        kept_mean = [sb("r%d" % t, [P, S], F32) for t in range(PACK - 1)]
+        kept_mean = [sb("r%d" % t, [P, S], F32)[:] for t in range(PAIR)] + [w1_raw_1[:, 0, :], keep[2][:]]
 
         def gather_kept_mean(t, first, last):
             nc.vector.tensor_tensor(
@@ -158,20 +184,20 @@ def tile_picked_ykal_mean_po_kernel(
             )
 
         w1a_first = round_pair("w1a", w1_raw_0, 0, nc.vector.tensor_copy)
+        w1a_second = round_pair("w1a", w1_raw_0, PAIR, nc.vector.tensor_copy)
         finish_keep(0)
         finish_keep(1)
         gather_kept_mean(0, 0, S)
-        w1a_second = round_pair("w1a", w1_raw_0, PAIR, nc.scalar.copy, decay[1])
         multiply_pass(y_banks[:PAIR], quantise_pair("w1a0", w1a_first), 0)
-        gather_kept_mean(1, 0, S)
         multiply_pass(y_banks[PAIR:], quantise_pair("w1a1", w1a_second), 0)
+        gather_kept_mean(1, 0, S)
         finish_keep(2)
         finish_keep(3)
         w1b_first = round_pair("w1b", w1_raw_1, 0, nc.vector.tensor_copy)
         w1b_second = round_pair("w1b", w1_raw_1, PAIR, nc.scalar.copy)
         multiply_pass(y_banks[:PAIR], quantise_pair("w1b0", w1b_first), 1)
-        gather_kept_mean(2, 0, S)
         multiply_pass(y_banks[PAIR:], quantise_pair("w1b1", w1b_second), 1)
+        gather_kept_mean(2, 0, S)
 
         out_rows = out_0.rearrange("(p t) s -> p t s", t=PACK)
         out_words = out_1[0].rearrange("p c r -> p (c r)").bitcast(I32)
@@ -188,8 +214,9 @@ def tile_picked_ykal_mean_po_kernel(
                 weighted_y[t][:, cols], keep[t][:, cols], 1.0, y_banks[t][:, cols], ALU.subtract, ALU.mult
             )
 
-        def difference(engine, t, h, kept):
-            engine.tensor_tensor(results[h][:, t, :], kept, weighted_y[t][:, halves[h]], ALU.subtract)
+        def difference(engine, t, h):
+            cols = halves[h]
+            engine.tensor_tensor(results[h][:, t, :], kept_mean[t][:, cols], weighted_y[t][:, cols], ALU.subtract)
 
         def store_pair(t0, h):
             rows = slice(t0, t0 + PAIR)
@@ -200,35 +227,23 @@ def tile_picked_ykal_mean_po_kernel(
             src = results[h][:].rearrange("p t (c i) -> p c t i", i=4)
             copy(dst[:, first // 4 : last // 4], src[:, first // 4 : last // 4])
 
-        def gather_last(out, h):
-            cols = halves[h]
-            nc.vector.tensor_tensor(
-                out, mean_tables[3][:].indirect(track_list[:, cols.start // 16 : cols.stop // 16]), keep[3][:, cols], ALU.mult
-            )
-
-        last_first_half = sb("r3", [P, HALF], F32)[:]
-        gather_last(last_first_half, 0)
-        weigh_y(0, 0)
-        weigh_y(1, 0)
-        difference(nc.gpsimd, 0, 0, kept_mean[0][:, halves[0]])
-        weigh_y(0, 1)
-        weigh_y(1, 1)
-        difference(nc.gpsimd, 1, 0, kept_mean[1][:, halves[0]])
+        for t0 in range(0, PACK, PAIR):
+            for h in range(2):
+                for t in range(t0, t0 + PAIR):
+                    weigh_y(t, h)
+        for t in range(PACK - 1):
+            difference(nc.gpsimd, t, 0)
         store_pair(0, 0)
-        weigh_y(2, 0)
-        weigh_y(3, 0)
-        difference(nc.vector, 2, 0, kept_mean[2][:, halves[0]])
-        difference(nc.vector, 3, 0, last_first_half)
+        gather_kept_mean(3, 0, HALF)
+        difference(nc.vector, 0, 1)
+        difference(nc.vector, 3, 0)
         store_pair(2, 0)
         round_columns(nc.scalar.copy, 0, 0, HALF)
-        weigh_y(2, 1)
-        weigh_y(3, 1)
-        difference(nc.gpsimd, 0, 1, kept_mean[0][:, halves[1]])
-        gather_last(last_first_half, 1)
-        difference(nc.vector, 1, 1, kept_mean[1][:, halves[1]])
+        gather_kept_mean(3, HALF, S)
+        difference(nc.vector, 1, 1)
         store_pair(0, 1)
-        difference(nc.vector, 2, 1, kept_mean[2][:, halves[1]])
-        difference(nc.vector, 3, 1, last_first_half)
+        difference(nc.vector, 2, 1)
+        difference(nc.vector, 3, 1)
         store_pair(2, 1)
         round_columns(nc.vector.tensor_copy, 1, 0, VECTOR_COLUMNS)
         round_columns(nc.scalar.copy, 1, VECTOR_COLUMNS, HALF)

@@ -173,7 +173,7 @@ def tile_picked_ykal_mean_po_kernel(
             nc.scalar.activation(decay[t][:], keep[t][:], ACT.Abs_reciprocal_sqrt, bias=1.0)
             nc.scalar.activation(keep[t][:], decay[t][:], ACT.Square)
 
-        kept_mean = [sb("r%d" % t, [P, S], F32)[:] for t in range(PAIR)] + [w1_raw_1[:, 0, :], keep[2][:]]
+        kept_mean = [sb("r%d" % t, [P, S], F32) for t in range(PACK - 1)] + [keep[2]]
 
         def gather_kept_mean(t, first, last):
             nc.vector.tensor_tensor(
@@ -196,8 +196,8 @@ def tile_picked_ykal_mean_po_kernel(
         w1b_first = round_pair("w1b", w1_raw_1, 0, nc.vector.tensor_copy)
         w1b_second = round_pair("w1b", w1_raw_1, PAIR, nc.scalar.copy)
         multiply_pass(y_banks[:PAIR], quantise_pair("w1b0", w1b_first), 1)
-        multiply_pass(y_banks[PAIR:], quantise_pair("w1b1", w1b_second), 1)
         gather_kept_mean(2, 0, S)
+        multiply_pass(y_banks[PAIR:], quantise_pair("w1b1", w1b_second), 1)
 
         out_rows = out_0.rearrange("(p t) s -> p t s", t=PACK)
         out_words = out_1[0].rearrange("p c r -> p (c r)").bitcast(I32)

@@ -196,8 +196,9 @@ def tile_picked_ykal_mean_po_kernel(
         w1b_first = round_pair("w1b", w1_raw_1, 0, nc.vector.tensor_copy)
         w1b_second = round_pair("w1b", w1_raw_1, PAIR, nc.scalar.copy)
         multiply_pass(y_banks[:PAIR], quantise_pair("w1b0", w1b_first), 1)
-        gather_kept_mean(2, 0, S)
+        gather_kept_mean(2, 0, HALF)
         multiply_pass(y_banks[PAIR:], quantise_pair("w1b1", w1b_second), 1)
+        gather_kept_mean(2, HALF, S)
 
         out_rows = out_0.rearrange("(p t) s -> p t s", t=PACK)
         out_words = out_1[0].rearrange("p c r -> p (c r)").bitcast(I32)
@@ -227,10 +228,12 @@ def tile_picked_ykal_mean_po_kernel(
             src = results[h][:].rearrange("p t (c i) -> p c t i", i=4)
             copy(dst[:, first // 4 : last // 4], src[:, first // 4 : last // 4])
 
-        for t0 in range(0, PACK, PAIR):
+        for h in range(2):
+            for t in range(PAIR):
+                weigh_y(t, h)
+        for t in range(PAIR, PACK):
             for h in range(2):
-                for t in range(t0, t0 + PAIR):
-                    weigh_y(t, h)
+                weigh_y(t, h)
         for t in range(PACK - 1):
             difference(nc.gpsimd, t, 0)
         store_pair(0, 0)

@@ -22,7 +22,7 @@ PASSES = K // K_PASS
 QUADRANTS = 4
 PAIR = 2
 HALF = S // 2
-VECTOR_COLUMNS = 144
+VECTOR_COLUMNS = 160
 GPSIMD_TILES = 3
 
 
@@ -215,9 +215,11 @@ def tile_picked_ykal_mean_po_kernel(
                 weighted_y[t][:, cols], keep[t][:, cols], 1.0, y_banks[t][:, cols], ALU.subtract, ALU.mult
             )
 
-        def difference(engine, t, h):
-            cols = halves[h]
-            engine.tensor_tensor(results[h][:, t, :], kept_mean[t][:, cols], weighted_y[t][:, cols], ALU.subtract)
+        def difference(engine, t, h, first=0, last=HALF):
+            cols = slice(h * HALF + first, h * HALF + last)
+            engine.tensor_tensor(
+                results[h][:, t, first:last], kept_mean[t][:, cols], weighted_y[t][:, cols], ALU.subtract
+            )
 
         def store_pair(t0, h):
             rows = slice(t0, t0 + PAIR)
@@ -245,8 +247,9 @@ def tile_picked_ykal_mean_po_kernel(
         gather_kept_mean(3, HALF, S)
         difference(nc.vector, 1, 1)
         store_pair(0, 1)
-        difference(nc.vector, 2, 1)
-        difference(nc.vector, 3, 1)
+        for first, last in ((0, VECTOR_COLUMNS), (VECTOR_COLUMNS, HALF)):
+            for t in range(PAIR, PACK):
+                difference(nc.vector, t, 1, first, last)
         store_pair(2, 1)
         round_columns(nc.vector.tensor_copy, 1, 0, VECTOR_COLUMNS)
         round_columns(nc.scalar.copy, 1, VECTOR_COLUMNS, HALF)

@@ -221,8 +221,8 @@ def tile_picked_ykal_mean_po_kernel(
                 results[h][:, t, first:last], kept_mean[t][:, cols], weighted_y[t][:, cols], ALU.subtract
             )
 
-        def store_pair(t0, h):
-            rows = slice(t0, t0 + PAIR)
+        def store_rows(first, last, h):
+            rows = slice(first, last)
             nc.sync.dma_start(out_rows[:, rows, halves[h]], results[h][:, rows, :])
 
         def round_columns(copy, h, first, last):
@@ -238,19 +238,19 @@ def tile_picked_ykal_mean_po_kernel(
                 weigh_y(t, h)
         for t in range(PACK - 1):
             difference(nc.gpsimd, t, 0)
-        store_pair(0, 0)
+        store_rows(0, 3, 0)
         gather_kept_mean(3, 0, HALF)
         difference(nc.vector, 0, 1)
         difference(nc.vector, 3, 0)
-        store_pair(2, 0)
+        store_rows(3, 4, 0)
         round_columns(nc.scalar.copy, 0, 0, HALF)
         gather_kept_mean(3, HALF, S)
         difference(nc.vector, 1, 1)
-        store_pair(0, 1)
+        store_rows(0, 2, 1)
         for first, last in ((0, VECTOR_COLUMNS), (VECTOR_COLUMNS, HALF)):
             for t in range(PAIR, PACK):
                 difference(nc.vector, t, 1, first, last)
-        store_pair(2, 1)
+        store_rows(2, 4, 1)
         round_columns(nc.vector.tensor_copy, 1, 0, VECTOR_COLUMNS)
         round_columns(nc.scalar.copy, 1, VECTOR_COLUMNS, HALF)
 

@@ -20,10 +20,13 @@ PACK = 4
 K_PASS = P * PACK
 PASSES = K // K_PASS
 QUADRANTS = 4
+LIST_ROWS = 16
 PAIR = 2
+BANKS = 8
 HALF = S // 2
+LAST = PACK - 1
+ROOT_UNIT = 2.0**-16
 VECTOR_COLUMNS = 160
-GPSIMD_TILES = 3
 
 
 def tile_picked_ykal_mean_po_kernel(
@@ -37,8 +40,11 @@ def tile_picked_ykal_mean_po_kernel(
         def sb(name, shape, dtype):
             return sbuf.tile(shape, dtype, name=name, align_bytes=64)
 
-        offs_list = sbuf.tile([P, S // 16], U16, name="offs_t")
-        track_list = sbuf.tile([P, S // 16], U16, name="track_t")
+        offs_list = sbuf.tile([P, S // LIST_ROWS], U16, name="offs_t")
+        track_list = sbuf.tile([P, S // LIST_ROWS], U16, name="track_t")
+
+        def picked(table, entries, first, last):
+            return table[:].indirect(entries[:, first // LIST_ROWS : last // LIST_ROWS])
 
         x_scale_table = sb("xs", [P, T], U8)
         nc.vector.memset(x_scale_table[:].bitcast(I32), 0)
@@ -54,12 +60,10 @@ def tile_picked_ykal_mean_po_kernel(
             return raw
 
         def load_row_tile(src, name, t):
-            table = sb(name, [P, U], F32)
+            table = sb("%s%d" % (name, t), [P, U], F32)
             nc.sync.dma_start(table[:], src.rearrange("(p t) u -> p t u", t=PACK)[:, t, :])
             return table
 
-        var_tables = []
-        mean_tables = []
         nc.sync.dma_start(offs_list[:], offs)
         word_table_0 = load_words(0)
         for quad in range(QUADRANTS):
@@ -68,57 +72,38 @@ def tile_picked_ykal_mean_po_kernel(
                 x_scales[:, 4 * quad : 4 * quad + 4, :].bitcast(I32),
             )
         nc.sync.dma_start(track_list[:], track)
-        w2_raw_0 = load_weight(w2, "w2a", 0)
-        w2_raw_1 = load_weight(w2, "w2b", 1)
+        w2_raw = [load_weight(w2, "w2_%d" % g, g) for g in range(PASSES)]
         word_table_1 = load_words(1)
-        var_tables.append(load_row_tile(var, "var0", 0))
-        var_tables.append(load_row_tile(var, "var1", 1))
-        var_tables.append(load_row_tile(var, "var2", 2))
-        var_tables.append(load_row_tile(var, "var3", 3))
-        w1_raw_0 = load_weight(w1, "w1a", 0)
-        mean_tables.append(load_row_tile(mean, "mean0", 0))
-        mean_tables.append(load_row_tile(mean, "mean1", 1))
-        w1_raw_1 = load_weight(w1, "w1b", 1)
-        mean_tables.append(load_row_tile(mean, "mean2", 2))
-        mean_tables.append(load_row_tile(mean, "mean3", 3))
+        var_tables = [load_row_tile(var, "var", t) for t in range(PACK)]
+        w1_raw = []
+        mean_tables = []
+        for g in range(PASSES):
+            w1_raw.append(load_weight(w1, "w1_%d" % g, g))
+            mean_tables.extend([load_row_tile(mean, "mean", t) for t in range(g * PAIR, (g + 1) * PAIR)])
 
         x_codes = [sb("xg%d" % g, [P, S], U32) for g in range(PASSES)]
-
-        def gather_words(g, table, first, last):
-            nc.vector.tensor_copy(x_codes[g][:, first:last], table[:].indirect(offs_list[:, first // 16 : last // 16]))
-
-        gather_words(0, word_table_0, 0, S)
+        nc.vector.tensor_copy(x_codes[0][:], picked(word_table_0, offs_list, 0, S))
         x_scale_bytes = sb("xsg", [P, S], U8)
-        nc.vector.tensor_copy(x_scale_bytes[:], x_scale_table[:].indirect(offs_list[:]))
+        nc.vector.tensor_copy(x_scale_bytes[:], picked(x_scale_table, offs_list, 0, S))
 
-        def round_pair(name, raw, t0, copy, reused=None):
-            if reused is None:
-                rounded = sb("%sb%d" % (name, t0), [P, PAIR * P * PACK], BF16)[:]
-            else:
-                rounded = reused[:].bitcast(BF16)
+        def round_pair(name, raw, t0, copy):
+            rounded = sb("%s_bf16_%d" % (name, t0), [P, PAIR * P * PACK], BF16)
             copy(
-                rounded.rearrange("p (t c j) -> p c j t", t=PAIR, j=PACK),
+                rounded[:].rearrange("p (t c j) -> p c j t", t=PAIR, j=PACK),
                 raw[:].rearrange("p j (c t) -> p c j t", t=PACK)[:, :, :, t0 : t0 + PAIR],
             )
             return rounded
 
         def quantise_pair(name, rounded):
-            codes = sb("%sc" % name, [P, PAIR * P], U32)
-            scales = sb("%ss" % name, [P, PAIR * P], U8)
-            nc.vector.quantize_mx(
-                out=codes[:].bitcast(FP8X4), scales=scales[:], in_=rounded
-            )
+            codes = sb("%s_codes" % name, [P, PAIR * P], U32)
+            scales = sb("%s_scales" % name, [P, PAIR * P], U8)
+            nc.vector.quantize_mx(out=codes[:].bitcast(FP8X4), scales=scales[:], in_=rounded[:])
             return [(codes[:, t * P : (t + 1) * P], scales[:, t * P : (t + 1) * P]) for t in range(PAIR)]
 
-        def quantise_pass(name, raw, first_copy, second_copy):
-            first = round_pair(name, raw, 0, first_copy)
-            second = round_pair(name, raw, PAIR, second_copy)
-            return quantise_pair(name + "0", first) + quantise_pair(name + "1", second)
-
-        def multiply(bank, weights, g, first=0, last=S):
-            codes, scales = weights
+        def multiply(bank, tile_weights, g, first=0, last=S):
+            codes, scales = tile_weights
             nc.tensor.matmul_mx(
-                out=bank,
+                out=bank[:],
                 lhsT=codes.bitcast(FP8X4),
                 lhsT_scale=scales,
                 rhs=x_codes[g][:, first:last].bitcast(FP8X4),
@@ -127,87 +112,94 @@ def tile_picked_ykal_mean_po_kernel(
                 stop=(g == PASSES - 1),
             )
 
-        def multiply_pass(banks, weights, g):
+        def multiply_tiles(banks, weights, g):
             for bank, tile_weights in zip(banks, weights):
-                multiply(bank[:], tile_weights, g)
+                multiply(bank, tile_weights, g)
 
+        spans = [(h * HALF, (h + 1) * HALF) for h in range(2)]
         z_halves = [psum.tile([P, HALF], F32, name="zh%d" % h, tag="bank%d" % h) for h in range(2)]
-        z_banks = [psum.tile([P, S], F32, name="z%d" % t, tag="bank%d" % (t + 1)) for t in range(1, PACK)]
+        z_others = [psum.tile([P, S], F32, name="z%d" % t, tag="bank%d" % (t + 1)) for t in range(1, PACK)]
 
-        w2_pass_0 = quantise_pass("w2a", w2_raw_0, nc.vector.tensor_copy, nc.scalar.copy)
-        for h in range(2):
-            multiply(z_halves[h][:], w2_pass_0[0], 0, h * HALF, (h + 1) * HALF)
-        multiply_pass(z_banks, w2_pass_0[1:], 0)
-        w2b_first = round_pair("w2b", w2_raw_1, 0, nc.vector.tensor_copy)
-        w2b_second = round_pair("w2b", w2_raw_1, PAIR, nc.scalar.copy)
-        w2_pass_1 = quantise_pair("w2b0", w2b_first)
-        gather_words(1, word_table_1, 0, HALF)
-        multiply(z_halves[0][:], w2_pass_1[0], 1, 0, HALF)
-        gather_words(1, word_table_1, HALF, S)
-        multiply(z_halves[1][:], w2_pass_1[0], 1, HALF, S)
-        w2_pass_1 = w2_pass_1 + quantise_pair("w2b1", w2b_second)
-        multiply_pass(z_banks, w2_pass_1[1:], 1)
+        w2_first_pair = round_pair("w2_0", w2_raw[0], 0, nc.vector.tensor_copy)
+        w2_second_pair = round_pair("w2_0", w2_raw[0], PAIR, nc.scalar.copy)
+        w2_pass = quantise_pair("w2_00", w2_first_pair) + quantise_pair("w2_01", w2_second_pair)
+        for bank, (first, last) in zip(z_halves, spans):
+            multiply(bank, w2_pass[0], 0, first, last)
+        multiply_tiles(z_others, w2_pass[1:], 0)
 
-        decay = [sb("e%d" % t, [P, S], F32) for t in range(PACK)]
-        keep = [sb("h%d" % t, [P, S], F32) for t in range(PACK)]
-        for h in range(2):
-            nc.scalar.activation(decay[0][:, h * HALF : (h + 1) * HALF], z_halves[h][:], ACT.Exp, scale=-1.0)
+        w2_first_pair = round_pair("w2_1", w2_raw[1], 0, nc.vector.tensor_copy)
+        w2_second_pair = round_pair("w2_1", w2_raw[1], PAIR, nc.scalar.copy)
+        w2_pass = quantise_pair("w2_10", w2_first_pair)
+        for bank, (first, last) in zip(z_halves, spans):
+            nc.vector.tensor_copy(x_codes[1][:, first:last], picked(word_table_1, offs_list, first, last))
+            multiply(bank, w2_pass[0], 1, first, last)
+        w2_pass = w2_pass + quantise_pair("w2_11", w2_second_pair)
+        multiply_tiles(z_others, w2_pass[1:], 1)
+
+        decay = [sb("decay%d" % t, [P, S], F32) for t in range(PACK)]
+        keep = [sb("keep%d" % t, [P, S], F32) for t in range(PACK)]
+        for bank, (first, last) in zip(z_halves, spans):
+            nc.scalar.activation(decay[0][:, first:last], bank[:], ACT.Exp, scale=-1.0)
         for t in range(1, PACK):
-            nc.scalar.activation(decay[t][:], z_banks[t - 1][:], ACT.Exp, scale=-1.0)
-        y_banks = [psum.tile([P, S], F32, name="y%d" % t, tag="bank%d" % ((t + PACK + 1) % (2 * PACK))) for t in range(PACK)]
+            nc.scalar.activation(decay[t][:], z_others[t - 1][:], ACT.Exp, scale=-1.0)
+        y_banks = [
+            psum.tile([P, S], F32, name="y%d" % t, tag="bank%d" % ((PACK + 1 + t) % BANKS)) for t in range(PACK)
+        ]
 
         def gather_ratio(t, first, last):
             nc.vector.tensor_tensor(
                 keep[t][:, first:last],
-                var_tables[t][:].indirect(track_list[:, first // 16 : last // 16]),
+                picked(var_tables[t], track_list, first, last),
                 decay[t][:, first:last],
                 ALU.mult,
             )
 
-        gather_ratio(0, 0, HALF)
-        gather_ratio(0, HALF, S)
+        for first, last in spans:
+            gather_ratio(0, first, last)
         for t in range(1, PACK):
             gather_ratio(t, 0, S)
 
         def finish_keep(t):
-            nc.scalar.activation(decay[t][:], keep[t][:], ACT.Abs_reciprocal_sqrt, bias=1.0)
-            nc.scalar.activation(keep[t][:], decay[t][:], ACT.Square)
+            nc.scalar.activation(
+                decay[t][:], keep[t][:], ACT.Abs_reciprocal_sqrt, scale=ROOT_UNIT**2, bias=ROOT_UNIT**2
+            )
+            nc.scalar.activation(keep[t][:], decay[t][:], ACT.Square, scale=ROOT_UNIT)
 
-        kept_mean = [sb("r%d" % t, [P, S], F32) for t in range(PACK - 1)] + [keep[2]]
+        kept_mean = [sb("kept_mean%d" % t, [P, S], F32) for t in range(LAST)] + [keep[LAST - 1]]
 
         def gather_kept_mean(t, first, last):
             nc.vector.tensor_tensor(
                 kept_mean[t][:, first:last],
-                mean_tables[t][:].indirect(track_list[:, first // 16 : last // 16]),
+                picked(mean_tables[t], track_list, first, last),
                 keep[t][:, first:last],
                 ALU.mult,
             )
 
-        w1a_first = round_pair("w1a", w1_raw_0, 0, nc.vector.tensor_copy)
-        w1a_second = round_pair("w1a", w1_raw_0, PAIR, nc.vector.tensor_copy)
-        finish_keep(0)
-        finish_keep(1)
+        w1_first_pair = round_pair("w1_0", w1_raw[0], 0, nc.vector.tensor_copy)
+        w1_second_pair = round_pair("w1_0", w1_raw[0], PAIR, nc.vector.tensor_copy)
+        for t in range(PAIR):
+            finish_keep(t)
         gather_kept_mean(0, 0, S)
-        multiply_pass(y_banks[:PAIR], quantise_pair("w1a0", w1a_first), 0)
-        multiply_pass(y_banks[PAIR:], quantise_pair("w1a1", w1a_second), 0)
+        multiply_tiles(y_banks[:PAIR], quantise_pair("w1_00", w1_first_pair), 0)
+        multiply_tiles(y_banks[PAIR:], quantise_pair("w1_01", w1_second_pair), 0)
         gather_kept_mean(1, 0, S)
-        finish_keep(2)
-        finish_keep(3)
-        w1b_first = round_pair("w1b", w1_raw_1, 0, nc.vector.tensor_copy)
-        w1b_second = round_pair("w1b", w1_raw_1, PAIR, nc.scalar.copy)
-        multiply_pass(y_banks[:PAIR], quantise_pair("w1b0", w1b_first), 1)
+        for t in range(PAIR, PACK):
+            finish_keep(t)
+        w1_first_pair = round_pair("w1_1", w1_raw[1], 0, nc.vector.tensor_copy)
+        w1_second_pair = round_pair("w1_1", w1_raw[1], PAIR, nc.scalar.copy)
+        multiply_tiles(y_banks[:PAIR], quantise_pair("w1_10", w1_first_pair), 1)
         gather_kept_mean(2, 0, HALF)
-        multiply_pass(y_banks[PAIR:], quantise_pair("w1b1", w1b_second), 1)
+        multiply_tiles(y_banks[PAIR:], quantise_pair("w1_11", w1_second_pair), 1)
         gather_kept_mean(2, HALF, S)
 
         out_rows = out_0.rearrange("(p t) s -> p t s", t=PACK)
         out_words = out_1[0].rearrange("p c r -> p (c r)").bitcast(I32)
-        result_codes = sb("oc", [P, S], U32)
-        result_scales = sb("osc", [P, S], U8)
-        halves = [slice(h * HALF, (h + 1) * HALF) for h in range(2)]
-        results = [sb("res%d" % h, [P, PACK, HALF], F32) for h in range(2)]
-        rounded_halves = [sb("rb%d" % h, [P, HALF, PACK], BF16) for h in range(2)]
-        weighted_y = [sb("p%d" % t, [P, S], F32) for t in range(PACK)]
+        result_codes = sb("result_codes", [P, S], U32)
+        result_scales = sb("result_scales", [P, S], U8)
+        halves = [slice(first, last) for first, last in spans]
+        results = [sb("result%d" % h, [P, PACK, HALF], F32) for h in range(2)]
+        rounded_results = [sb("result_bf16_%d" % h, [P, HALF, PACK], BF16) for h in range(2)]
+        weighted_y = [sb("weighted_y%d" % t, [P, S], F32) for t in range(PACK)]
 
         def weigh_y(t, h):
             cols = halves[h]
@@ -221,12 +213,12 @@ def tile_picked_ykal_mean_po_kernel(
                 results[h][:, t, first:last], kept_mean[t][:, cols], weighted_y[t][:, cols], ALU.subtract
             )
 
-        def store_rows(first, last, h):
-            rows = slice(first, last)
+        def store_rows(first_tile, last_tile, h):
+            rows = slice(first_tile, last_tile)
             nc.sync.dma_start(out_rows[:, rows, halves[h]], results[h][:, rows, :])
 
         def round_columns(copy, h, first, last):
-            dst = rounded_halves[h][:].rearrange("p (c i) t -> p c t i", i=4)
+            dst = rounded_results[h][:].rearrange("p (c i) t -> p c t i", i=4)
             src = results[h][:].rearrange("p t (c i) -> p c t i", i=4)
             copy(dst[:, first // 4 : last // 4], src[:, first // 4 : last // 4])
 
@@ -236,25 +228,27 @@ def tile_picked_ykal_mean_po_kernel(
         for t in range(PAIR, PACK):
             for h in range(2):
                 weigh_y(t, h)
-        for t in range(PACK - 1):
+        for t in range(LAST):
             difference(nc.gpsimd, t, 0)
-        store_rows(0, 3, 0)
-        gather_kept_mean(3, 0, HALF)
+        store_rows(0, LAST, 0)
+
+        gather_kept_mean(LAST, 0, HALF)
         difference(nc.vector, 0, 1)
-        difference(nc.vector, 3, 0)
-        store_rows(3, 4, 0)
+        difference(nc.vector, LAST, 0)
+        store_rows(LAST, PACK, 0)
         round_columns(nc.scalar.copy, 0, 0, HALF)
-        gather_kept_mean(3, HALF, S)
+
+        gather_kept_mean(LAST, HALF, S)
         difference(nc.vector, 1, 1)
-        store_rows(0, 2, 1)
+        store_rows(0, PAIR, 1)
         for first, last in ((0, VECTOR_COLUMNS), (VECTOR_COLUMNS, HALF)):
             for t in range(PAIR, PACK):
                 difference(nc.vector, t, 1, first, last)
-        store_rows(2, 4, 1)
+        store_rows(PAIR, PACK, 1)
         round_columns(nc.vector.tensor_copy, 1, 0, VECTOR_COLUMNS)
         round_columns(nc.scalar.copy, 1, VECTOR_COLUMNS, HALF)
 
-        for rounded, cols in zip(rounded_halves, halves):
+        for rounded, cols in zip(rounded_results, halves):
             nc.vector.quantize_mx(
                 out=result_codes[:, cols].bitcast(FP8X4),
                 scales=result_scales[:, cols],

@@ -1,6 +1,7 @@
 from contextlib import ExitStack
 
 import concourse.mybir as mybir
+from concourse.masks import make_identity
 
 K, T, S, N, U = 1024, 1024, 512, 512, 1024
 FLOPS = 2 * 2 * K * N * S
@@ -37,8 +38,8 @@ def tile_picked_ykal_mean_po_kernel(
         sbuf = ctx.enter_context(tc.tile_pool(name="keep", bufs=1))
         psum = ctx.enter_context(tc.psum_pool(name="psum", bufs=1))
 
-        def sb(name, shape, dtype):
-            return sbuf.tile(shape, dtype, name=name, align_bytes=64)
+        def sb(name, shape, dtype, tag=None):
+            return sbuf.tile(shape, dtype, name=name, tag=tag or name, align_bytes=64)
 
         offs_list = sbuf.tile([P, S // LIST_ROWS], U16, name="offs_t")
         track_list = sbuf.tile([P, S // LIST_ROWS], U16, name="track_t")
@@ -64,8 +65,8 @@ def tile_picked_ykal_mean_po_kernel(
             nc.sync.dma_start(table[:], src.rearrange("(p t) u -> p t u", t=PACK)[:, t, :])
             return table
 
-        nc.sync.dma_start(offs_list[:], offs)
         word_table_0 = load_words(0)
+        nc.sync.dma_start(offs_list[:], offs)
         for quad in range(QUADRANTS):
             nc.sync.dma_start(
                 x_scale_table[32 * quad : 32 * quad + 4 * PASSES, :].bitcast(I32),
@@ -74,12 +75,20 @@ def tile_picked_ykal_mean_po_kernel(
         nc.sync.dma_start(track_list[:], track)
         w2_raw = [load_weight(w2, "w2_%d" % g, g) for g in range(PASSES)]
         word_table_1 = load_words(1)
+        w1_raw = [load_weight(w1, "w1_0", 0)]
         var_tables = [load_row_tile(var, "var", t) for t in range(PACK)]
-        w1_raw = []
-        mean_tables = []
-        for g in range(PASSES):
-            w1_raw.append(load_weight(w1, "w1_%d" % g, g))
-            mean_tables.extend([load_row_tile(mean, "mean", t) for t in range(g * PAIR, (g + 1) * PAIR)])
+        mean_tables = [load_row_tile(mean, "mean", 0)]
+        w1_raw.append(load_weight(w1, "w1_1", 1))
+        mean_tables.extend([load_row_tile(mean, "mean", t) for t in range(1, PACK)])
+
+        identity = sb("identity", [P, P], F32)
+        make_identity(nc, identity[:])
+
+        def negate_on_vector(dst, src):
+            nc.vector.tensor_scalar(dst, src, -1.0, None, ALU.mult)
+
+        def negate_on_scalar(dst, src):
+            nc.scalar.activation(dst, src, ACT.Copy, scale=-1.0)
 
         x_codes = [sb("xg%d" % g, [P, S], U32) for g in range(PASSES)]
         nc.vector.tensor_copy(x_codes[0][:], picked(word_table_0, offs_list, 0, S))
@@ -136,34 +145,31 @@ def tile_picked_ykal_mean_po_kernel(
         w2_pass = w2_pass + quantise_pair("w2_11", w2_second_pair)
         multiply_tiles(z_others, w2_pass[1:], 1)
 
-        decay = [sb("decay%d" % t, [P, S], F32) for t in range(PACK)]
+        decay = [sb("decay%d" % t, [P, S], F32)[:] for t in range(PACK)]
+        roots = decay[:PAIR] + [w1_raw[1][:, t, :] for t in range(PAIR, PACK)]
         keep = [sb("keep%d" % t, [P, S], F32) for t in range(PACK)]
         for bank, (first, last) in zip(z_halves, spans):
             nc.scalar.activation(decay[0][:, first:last], bank[:], ACT.Exp, scale=-1.0)
+        w1_first_pair = round_pair("w1_0", w1_raw[0], 0, negate_on_vector)
+        w1_second_pair = round_pair("w1_0", w1_raw[0], PAIR, negate_on_vector)
         for t in range(1, PACK):
-            nc.scalar.activation(decay[t][:], z_others[t - 1][:], ACT.Exp, scale=-1.0)
+            nc.scalar.activation(decay[t], z_others[t - 1][:], ACT.Exp, scale=-1.0)
         y_banks = [
             psum.tile([P, S], F32, name="y%d" % t, tag="bank%d" % ((PACK + 1 + t) % BANKS)) for t in range(PACK)
         ]
 
-        def gather_ratio(t, first, last):
-            nc.vector.tensor_tensor(
-                keep[t][:, first:last],
-                picked(var_tables[t], track_list, first, last),
-                decay[t][:, first:last],
-                ALU.mult,
-            )
+        def gather_ratio(t):
+            nc.vector.tensor_tensor(keep[t][:], picked(var_tables[t], track_list, 0, S), decay[t], ALU.mult)
 
-        for first, last in spans:
-            gather_ratio(0, first, last)
+        gather_ratio(0)
+        multiply_tiles(y_banks[:PAIR], quantise_pair("w1_00", w1_first_pair), 0)
+        multiply_tiles(y_banks[PAIR:], quantise_pair("w1_01", w1_second_pair), 0)
         for t in range(1, PACK):
-            gather_ratio(t, 0, S)
+            gather_ratio(t)
 
         def finish_keep(t):
-            nc.scalar.activation(
-                decay[t][:], keep[t][:], ACT.Abs_reciprocal_sqrt, scale=ROOT_UNIT**2, bias=ROOT_UNIT**2
-            )
-            nc.scalar.activation(keep[t][:], decay[t][:], ACT.Square, scale=ROOT_UNIT)
+            nc.scalar.activation(roots[t], keep[t][:], ACT.Abs_reciprocal_sqrt, scale=ROOT_UNIT**2, bias=ROOT_UNIT**2)
+            nc.scalar.activation(keep[t][:], roots[t], ACT.Square, scale=ROOT_UNIT)
 
         kept_mean = [sb("kept_mean%d" % t, [P, S], F32) for t in range(LAST)] + [keep[LAST - 1]]
 
@@ -175,76 +181,89 @@ def tile_picked_ykal_mean_po_kernel(
                 ALU.mult,
             )
 
-        w1_first_pair = round_pair("w1_0", w1_raw[0], 0, nc.vector.tensor_copy)
-        w1_second_pair = round_pair("w1_0", w1_raw[0], PAIR, nc.vector.tensor_copy)
         for t in range(PAIR):
             finish_keep(t)
         gather_kept_mean(0, 0, S)
-        multiply_tiles(y_banks[:PAIR], quantise_pair("w1_00", w1_first_pair), 0)
-        multiply_tiles(y_banks[PAIR:], quantise_pair("w1_01", w1_second_pair), 0)
-        gather_kept_mean(1, 0, S)
+        w1_first_pair = round_pair("w1_1", w1_raw[1], 0, negate_on_vector)
+        w1_second_pair = round_pair("w1_1", w1_raw[1], PAIR, negate_on_scalar)
         for t in range(PAIR, PACK):
             finish_keep(t)
-        w1_first_pair = round_pair("w1_1", w1_raw[1], 0, nc.vector.tensor_copy)
-        w1_second_pair = round_pair("w1_1", w1_raw[1], PAIR, nc.scalar.copy)
         multiply_tiles(y_banks[:PAIR], quantise_pair("w1_10", w1_first_pair), 1)
-        gather_kept_mean(2, 0, HALF)
+        gather_kept_mean(1, 0, S)
         multiply_tiles(y_banks[PAIR:], quantise_pair("w1_11", w1_second_pair), 1)
-        gather_kept_mean(2, HALF, S)
 
         out_rows = out_0.rearrange("(p t) s -> p t s", t=PACK)
         out_words = out_1[0].rearrange("p c r -> p (c r)").bitcast(I32)
         result_codes = sb("result_codes", [P, S], U32)
         result_scales = sb("result_scales", [P, S], U8)
         halves = [slice(first, last) for first, last in spans]
-        results = [sb("result%d" % h, [P, PACK, HALF], F32) for h in range(2)]
         rounded_results = [sb("result_bf16_%d" % h, [P, HALF, PACK], BF16) for h in range(2)]
         weighted_y = [sb("weighted_y%d" % t, [P, S], F32) for t in range(PACK)]
 
-        def weigh_y(t, h):
-            cols = halves[h]
-            nc.vector.scalar_tensor_tensor(
-                weighted_y[t][:, cols], keep[t][:, cols], 1.0, y_banks[t][:, cols], ALU.subtract, ALU.mult
-            )
+        def weigh_y(t):
+            for cols in halves:
+                nc.vector.scalar_tensor_tensor(
+                    weighted_y[t][:, cols], keep[t][:, cols], 1.0, y_banks[t][:, cols], ALU.subtract, ALU.mult
+                )
 
-        def difference(engine, t, h, first=0, last=HALF):
-            cols = slice(h * HALF + first, h * HALF + last)
+        def add_on_tensor(t):
+            turned = psum.tile([P, S], F32, name="turned", tag="bank1")
+            blocks = S // P
+            for n, term in enumerate((kept_mean[t], weighted_y[t])):
+                for b in range(blocks):
+                    cols = slice(b * P, (b + 1) * P)
+                    nc.tensor.matmul(
+                        turned[:, cols],
+                        term[:, cols],
+                        identity[:],
+                        start=(n == 0 and b == 0),
+                        stop=(n == 1 and b == blocks - 1),
+                        is_transpose=True,
+                    )
+            turned_sum = sb("turned_sum", [P, S], F32)
+            nc.scalar.copy(turned_sum[:], turned[:])
+            upright = psum.tile([P, S], F32, name="upright", tag="bank2")
+            for b in range(blocks):
+                cols = slice(b * P, (b + 1) * P)
+                nc.tensor.transpose(upright[:, cols], turned_sum[:, cols], identity[:])
+            return upright
+
+        weigh_y(0)
+        first_sum = add_on_tensor(0)
+        weigh_y(1)
+        gather_kept_mean(2, 0, S)
+        result = sb("result", [P, PACK, S], F32, "mean2")
+
+        def add_terms(engine, t, first, last):
             engine.tensor_tensor(
-                results[h][:, t, first:last], kept_mean[t][:, cols], weighted_y[t][:, cols], ALU.subtract
+                result[:, t, first:last], kept_mean[t][:, first:last], weighted_y[t][:, first:last], ALU.add
             )
 
-        def store_rows(first_tile, last_tile, h):
-            rows = slice(first_tile, last_tile)
-            nc.sync.dma_start(out_rows[:, rows, halves[h]], results[h][:, rows, :])
+        def store_rows(first_tile, last_tile, first, last):
+            nc.sync.dma_start(out_rows[:, first_tile:last_tile, first:last], result[:, first_tile:last_tile, first:last])
 
         def round_columns(copy, h, first, last):
             dst = rounded_results[h][:].rearrange("p (c i) t -> p c t i", i=4)
-            src = results[h][:].rearrange("p t (c i) -> p c t i", i=4)
+            src = result[:, :, halves[h]].rearrange("p t (c i) -> p c t i", i=4)
             copy(dst[:, first // 4 : last // 4], src[:, first // 4 : last // 4])
 
-        for h in range(2):
-            for t in range(PAIR):
-                weigh_y(t, h)
+        add_terms(nc.gpsimd, 1, 0, S)
+        store_rows(1, 2, 0, S)
+        nc.scalar.copy(result[:, 0, :], first_sum[:])
+        store_rows(0, 1, 0, S)
         for t in range(PAIR, PACK):
-            for h in range(2):
-                weigh_y(t, h)
-        for t in range(LAST):
-            difference(nc.gpsimd, t, 0)
-        store_rows(0, LAST, 0)
+            weigh_y(t)
 
         gather_kept_mean(LAST, 0, HALF)
-        difference(nc.vector, 0, 1)
-        difference(nc.vector, LAST, 0)
-        store_rows(LAST, PACK, 0)
+        for t in range(PAIR, PACK):
+            add_terms(nc.vector, t, 0, HALF)
+        store_rows(PAIR, PACK, 0, HALF)
         round_columns(nc.scalar.copy, 0, 0, HALF)
-
         gather_kept_mean(LAST, HALF, S)
-        difference(nc.vector, 1, 1)
-        store_rows(0, PAIR, 1)
-        for first, last in ((0, VECTOR_COLUMNS), (VECTOR_COLUMNS, HALF)):
+        for first, last in ((HALF, HALF + VECTOR_COLUMNS), (HALF + VECTOR_COLUMNS, S)):
             for t in range(PAIR, PACK):
-                difference(nc.vector, t, 1, first, last)
-        store_rows(PAIR, PACK, 1)
+                add_terms(nc.vector, t, first, last)
+        store_rows(PAIR, PACK, HALF, S)
         round_columns(nc.vector.tensor_copy, 1, 0, VECTOR_COLUMNS)
         round_columns(nc.scalar.copy, 1, VECTOR_COLUMNS, HALF)
 

@@ -190,7 +190,6 @@ def tile_picked_ykal_mean_po_kernel(
             finish_keep(t)
         multiply_tiles(y_banks[:PAIR], quantise_pair("w1_10", w1_first_pair), 1)
         gather_kept_mean(1, 0, S)
-        multiply_tiles(y_banks[PAIR:], quantise_pair("w1_11", w1_second_pair), 1)
 
         out_rows = out_0.rearrange("(p t) s -> p t s", t=PACK)
         out_words = out_1[0].rearrange("p c r -> p (c r)").bitcast(I32)
@@ -200,70 +199,76 @@ def tile_picked_ykal_mean_po_kernel(
         rounded_results = [sb("result_bf16_%d" % h, [P, HALF, PACK], BF16) for h in range(2)]
         weighted_y = [sb("weighted_y%d" % t, [P, S], F32) for t in range(PACK)]
 
-        def weigh_y(t):
-            for cols in halves:
-                nc.vector.scalar_tensor_tensor(
-                    weighted_y[t][:, cols], keep[t][:, cols], 1.0, y_banks[t][:, cols], ALU.subtract, ALU.mult
-                )
-
-        def add_on_tensor(t):
-            turned = psum.tile([P, S], F32, name="turned", tag="bank1")
-            blocks = S // P
-            for n, term in enumerate((kept_mean[t], weighted_y[t])):
-                for b in range(blocks):
-                    cols = slice(b * P, (b + 1) * P)
-                    nc.tensor.matmul(
-                        turned[:, cols],
-                        term[:, cols],
-                        identity[:],
-                        start=(n == 0 and b == 0),
-                        stop=(n == 1 and b == blocks - 1),
-                        is_transpose=True,
-                    )
-            turned_sum = sb("turned_sum", [P, S], F32)
-            nc.scalar.copy(turned_sum[:], turned[:])
-            upright = psum.tile([P, S], F32, name="upright", tag="bank2")
-            for b in range(blocks):
-                cols = slice(b * P, (b + 1) * P)
-                nc.tensor.transpose(upright[:, cols], turned_sum[:, cols], identity[:])
-            return upright
-
-        weigh_y(0)
-        first_sum = add_on_tensor(0)
-        weigh_y(1)
-        gather_kept_mean(2, 0, S)
-        result = sb("result", [P, PACK, S], F32, "mean2")
-
-        def add_terms(engine, t, first, last):
-            engine.tensor_tensor(
-                result[:, t, first:last], kept_mean[t][:, first:last], weighted_y[t][:, first:last], ALU.add
+        def weigh_y(t, h):
+            cols = halves[h]
+            nc.vector.scalar_tensor_tensor(
+                weighted_y[t][:, cols], keep[t][:, cols], 1.0, y_banks[t][:, cols], ALU.subtract, ALU.mult
             )
 
-        def store_rows(first_tile, last_tile, first, last):
-            nc.sync.dma_start(out_rows[:, first_tile:last_tile, first:last], result[:, first_tile:last_tile, first:last])
+        def add_on_tensor(t):
+            blocks = HALF // P
+            sums = []
+            for h, (first, last) in enumerate(spans):
+                turned = psum.tile([P, HALF], F32, name="turned%d" % h, tag="bank%d" % (1 + h))
+                for n, term in enumerate((kept_mean[t], weighted_y[t])):
+                    for b in range(blocks):
+                        nc.tensor.matmul(
+                            turned[:, b * P : (b + 1) * P],
+                            term[:, first + b * P : first + (b + 1) * P],
+                            identity[:],
+                            start=(n == 0 and b == 0),
+                            stop=(n == 1 and b == blocks - 1),
+                            is_transpose=True,
+                        )
+                turned_sum = sb("turned_sum%d" % h, [P, HALF], F32)
+                nc.scalar.copy(turned_sum[:], turned[:])
+                upright = psum.tile([P, HALF], F32, name="upright%d" % h, tag="bank%d" % (3 + h))
+                for b in range(blocks):
+                    cols = slice(b * P, (b + 1) * P)
+                    nc.tensor.transpose(upright[:, cols], turned_sum[:, cols], identity[:])
+                sums.append(upright)
+            return sums
+
+        results = [sb("result0", [P, PACK, HALF], F32)]
+
+        def add_terms(engine, t, h, first=0, last=HALF):
+            cols = slice(h * HALF + first, h * HALF + last)
+            engine.tensor_tensor(results[h][:, t, first:last], kept_mean[t][:, cols], weighted_y[t][:, cols], ALU.add)
+
+        def store_rows(first_tile, last_tile, h):
+            rows = slice(first_tile, last_tile)
+            nc.sync.dma_start(out_rows[:, rows, halves[h]], results[h][:, rows, :])
 
         def round_columns(copy, h, first, last):
             dst = rounded_results[h][:].rearrange("p (c i) t -> p c t i", i=4)
-            src = result[:, :, halves[h]].rearrange("p t (c i) -> p c t i", i=4)
+            src = results[h][:].rearrange("p t (c i) -> p c t i", i=4)
             copy(dst[:, first // 4 : last // 4], src[:, first // 4 : last // 4])
 
-        add_terms(nc.gpsimd, 1, 0, S)
-        store_rows(1, 2, 0, S)
-        nc.scalar.copy(result[:, 0, :], first_sum[:])
-        store_rows(0, 1, 0, S)
+        multiply_tiles(y_banks[PAIR:], quantise_pair("w1_11", w1_second_pair), 1)
+        for t, h in ((0, 0), (1, 0), (1, 1), (0, 1)):
+            weigh_y(t, h)
+        add_terms(nc.gpsimd, 0, 0)
+        first_sums = add_on_tensor(1)
+        gather_kept_mean(2, 0, S)
+        results.append(sb("result1", [P, PACK, HALF], F32, "mean2"))
+        add_terms(nc.gpsimd, 0, 1)
+        for h in range(2):
+            nc.scalar.copy(results[h][:, 1, :], first_sums[h][:])
+            store_rows(0, PAIR, h)
         for t in range(PAIR, PACK):
-            weigh_y(t)
+            for h in range(2):
+                weigh_y(t, h)
 
         gather_kept_mean(LAST, 0, HALF)
         for t in range(PAIR, PACK):
-            add_terms(nc.vector, t, 0, HALF)
-        store_rows(PAIR, PACK, 0, HALF)
+            add_terms(nc.vector, t, 0)
+        store_rows(PAIR, PACK, 0)
         round_columns(nc.scalar.copy, 0, 0, HALF)
         gather_kept_mean(LAST, HALF, S)
-        for first, last in ((HALF, HALF + VECTOR_COLUMNS), (HALF + VECTOR_COLUMNS, S)):
+        for first, last in ((0, VECTOR_COLUMNS), (VECTOR_COLUMNS, HALF)):
             for t in range(PAIR, PACK):
-                add_terms(nc.vector, t, first, last)
-        store_rows(PAIR, PACK, HALF, S)
+                add_terms(nc.vector, t, 1, first, last)
+        store_rows(PAIR, PACK, 1)
         round_columns(nc.vector.tensor_copy, 1, 0, VECTOR_COLUMNS)
         round_columns(nc.scalar.copy, 1, VECTOR_COLUMNS, HALF)
 

@@ -28,6 +28,7 @@ HALF = S // 2
 LAST = PACK - 1
 ROOT_UNIT = 2.0**-16
 VECTOR_COLUMNS = 160
+EARLY_SCALE_LOADS = 5
 
 
 def tile_picked_ykal_mean_po_kernel(
@@ -65,15 +66,23 @@ def tile_picked_ykal_mean_po_kernel(
             nc.sync.dma_start(table[:], src.rearrange("(p t) u -> p t u", t=PACK)[:, t, :])
             return table
 
+        def load_scale_rows(g, quad):
+            first = 32 * quad + 4 * g
+            nc.sync.dma_start(
+                x_scale_table[first : first + 4, :].bitcast(I32),
+                x_scales[g, 4 * quad : 4 * quad + 4, :].bitcast(I32),
+            )
+
+        scale_loads = [(g, quad) for g in range(PASSES) for quad in range(QUADRANTS)]
         word_table_0 = load_words(0)
         nc.sync.dma_start(offs_list[:], offs)
-        for quad in range(QUADRANTS):
-            nc.sync.dma_start(
-                x_scale_table[32 * quad : 32 * quad + 4 * PASSES, :].bitcast(I32),
-                x_scales[:, 4 * quad : 4 * quad + 4, :].bitcast(I32),
-            )
+        for g, quad in scale_loads[:EARLY_SCALE_LOADS]:
+            load_scale_rows(g, quad)
+        w2_raw = [load_weight(w2, "w2_0", 0)]
+        for g, quad in scale_loads[EARLY_SCALE_LOADS:]:
+            load_scale_rows(g, quad)
+        w2_raw.append(load_weight(w2, "w2_1", 1))
         nc.sync.dma_start(track_list[:], track)
-        w2_raw = [load_weight(w2, "w2_%d" % g, g) for g in range(PASSES)]
         word_table_1 = load_words(1)
         w1_raw = [load_weight(w1, "w1_0", 0)]
         var_tables = [load_row_tile(var, "var", t) for t in range(PACK)]
@@ -103,10 +112,11 @@ def tile_picked_ykal_mean_po_kernel(
             )
             return rounded
 
-        def quantise_pair(name, rounded):
-            codes = sb("%s_codes" % name, [P, PAIR * P], U32)
+        def quantise_pair(name, rounded, codes=None):
+            if codes is None:
+                codes = sb("%s_codes" % name, [P, PAIR * P], U32)[:]
             scales = sb("%s_scales" % name, [P, PAIR * P], U8)
-            nc.vector.quantize_mx(out=codes[:].bitcast(FP8X4), scales=scales[:], in_=rounded[:])
+            nc.vector.quantize_mx(out=codes.bitcast(FP8X4), scales=scales[:], in_=rounded[:])
             return [(codes[:, t * P : (t + 1) * P], scales[:, t * P : (t + 1) * P]) for t in range(PAIR)]
 
         def multiply(bank, tile_weights, g, first=0, last=S):
@@ -131,7 +141,9 @@ def tile_picked_ykal_mean_po_kernel(
 
         w2_first_pair = round_pair("w2_0", w2_raw[0], 0, nc.vector.tensor_copy)
         w2_second_pair = round_pair("w2_0", w2_raw[0], PAIR, nc.scalar.copy)
-        w2_pass = quantise_pair("w2_00", w2_first_pair) + quantise_pair("w2_01", w2_second_pair)
+        first_codes = sb("w2_0_codes", [P, PACK * P], U32, "xs")
+        w2_pass = quantise_pair("w2_00", w2_first_pair, first_codes[:, : PAIR * P])
+        w2_pass = w2_pass + quantise_pair("w2_01", w2_second_pair, first_codes[:, PAIR * P :])
         for bank, (first, last) in zip(z_halves, spans):
             multiply(bank, w2_pass[0], 0, first, last)
         multiply_tiles(z_others, w2_pass[1:], 0)

@@ -66,25 +66,24 @@ def tile_picked_ykal_mean_po_kernel(
             nc.sync.dma_start(table[:], src.rearrange("(p t) u -> p t u", t=PACK)[:, t, :])
             return table
 
-        def load_scale_rows(g, quad):
-            first = 32 * quad + 4 * g
+        def load_scale_rows(g, row):
             nc.sync.dma_start(
-                x_scale_table[first : first + 4, :].bitcast(I32),
-                x_scales[g, 4 * quad : 4 * quad + 4, :].bitcast(I32),
+                x_scale_table[4 * g + row : P : 32, :].bitcast(I32),
+                x_scales[g, row : 4 * QUADRANTS : 4, :].bitcast(I32),
             )
 
-        scale_loads = [(g, quad) for g in range(PASSES) for quad in range(QUADRANTS)]
+        scale_loads = [(g, row) for row in range(4) for g in range(PASSES)]
         word_table_0 = load_words(0)
         nc.sync.dma_start(offs_list[:], offs)
-        for g, quad in scale_loads[:EARLY_SCALE_LOADS]:
-            load_scale_rows(g, quad)
+        for g, row in scale_loads[:EARLY_SCALE_LOADS]:
+            load_scale_rows(g, row)
         w2_raw = [load_weight(w2, "w2_0", 0)]
-        for g, quad in scale_loads[EARLY_SCALE_LOADS:]:
-            load_scale_rows(g, quad)
+        for g, row in scale_loads[EARLY_SCALE_LOADS:]:
+            load_scale_rows(g, row)
         w2_raw.append(load_weight(w2, "w2_1", 1))
-        nc.sync.dma_start(track_list[:], track)
         word_table_1 = load_words(1)
         w1_raw = [load_weight(w1, "w1_0", 0)]
+        nc.sync.dma_start(track_list[:], track)
         var_tables = [load_row_tile(var, "var", t) for t in range(PACK)]
         mean_tables = [load_row_tile(mean, "mean", 0)]
         w1_raw.append(load_weight(w1, "w1_1", 1))

@@ -28,7 +28,7 @@ HALF = S // 2
 LAST = PACK - 1
 ROOT_UNIT = 2.0**-16
 VECTOR_COLUMNS = 160
-EARLY_SCALE_LOADS = 5
+EARLY_SCALE_LOADS = 2
 
 
 def tile_picked_ykal_mean_po_kernel(

@@ -27,7 +27,7 @@ BANKS = 8
 HALF = S // 2
 LAST = PACK - 1
 ROOT_UNIT = 2.0**-16
-VECTOR_COLUMNS = 160
+VECTOR_COLUMNS = 192
 EARLY_SCALE_LOADS = 2
 
 
@@ -103,19 +103,27 @@ def tile_picked_ykal_mean_po_kernel(
         x_scale_bytes = sb("xsg", [P, S], U8)
         nc.vector.tensor_copy(x_scale_bytes[:], picked(x_scale_table, offs_list, 0, S))
 
-        def round_pair(name, raw, t0, copy):
+        def round_pair(name, raw, t0, copy, calls=1):
             rounded = sb("%s_bf16_%d" % (name, t0), [P, PAIR * P * PACK], BF16)
-            copy(
-                rounded[:].rearrange("p (t c j) -> p c j t", t=PAIR, j=PACK),
-                raw[:].rearrange("p j (c t) -> p c j t", t=PACK)[:, :, :, t0 : t0 + PAIR],
-            )
+            dst = rounded[:].rearrange("p (t c j) -> p c j t", t=PAIR, j=PACK)
+            src = raw[:].rearrange("p j (c t) -> p c j t", t=PACK)[:, :, :, t0 : t0 + PAIR]
+            width = P // calls
+            for first in range(0, P, width):
+                copy(dst[:, first : first + width], src[:, first : first + width])
             return rounded
 
-        def quantise_pair(name, rounded, codes=None):
+        def quantise_pair(name, rounded, codes=None, order=None):
             if codes is None:
                 codes = sb("%s_codes" % name, [P, PAIR * P], U32)[:]
             scales = sb("%s_scales" % name, [P, PAIR * P], U8)
-            nc.vector.quantize_mx(out=codes.bitcast(FP8X4), scales=scales[:], in_=rounded[:])
+            width = PAIR * P // len(order or [0])
+            for piece in order or [0]:
+                cols = slice(piece * width, (piece + 1) * width)
+                nc.vector.quantize_mx(
+                    out=codes[:, cols].bitcast(FP8X4),
+                    scales=scales[:, cols],
+                    in_=rounded[:, PACK * piece * width : PACK * (piece + 1) * width],
+                )
             return [(codes[:, t * P : (t + 1) * P], scales[:, t * P : (t + 1) * P]) for t in range(PAIR)]
 
         def multiply(bank, tile_weights, g, first=0, last=S):
@@ -195,11 +203,11 @@ def tile_picked_ykal_mean_po_kernel(
         for t in range(PAIR):
             finish_keep(t)
         gather_kept_mean(0, 0, S)
-        w1_first_pair = round_pair("w1_1", w1_raw[1], 0, negate_on_vector)
+        w1_first_pair = round_pair("w1_1", w1_raw[1], 0, negate_on_vector, 2)
         w1_second_pair = round_pair("w1_1", w1_raw[1], PAIR, negate_on_scalar)
         for t in range(PAIR, PACK):
             finish_keep(t)
-        multiply_tiles(y_banks[:PAIR], quantise_pair("w1_10", w1_first_pair), 1)
+        multiply_tiles(y_banks[:PAIR], quantise_pair("w1_10", w1_first_pair, None, [0, 2, 1, 3]), 1)
         gather_kept_mean(1, 0, S)
 
         out_rows = out_0.rearrange("(p t) s -> p t s", t=PACK)

@@ -165,8 +165,7 @@ def tile_picked_ykal_mean_po_kernel(
         multiply_tiles(z_others, w2_pass[1:], 1)
 
         decay = [sb("decay%d" % t, [P, S], F32)[:] for t in range(PACK)]
-        roots = decay[:PAIR] + [w1_raw[1][:, t, :] for t in range(PAIR, PACK)]
-        keep = [sb("keep%d" % t, [P, S], F32) for t in range(PACK)]
+        ratio = [sb("ratio%d" % t, [P, S], F32) for t in range(PACK)]
         for bank, (first, last) in zip(z_halves, spans):
             nc.scalar.activation(decay[0][:, first:last], bank[:], ACT.Exp, scale=-1.0)
         w1_first_pair = round_pair("w1_0", w1_raw[0], 0, negate_on_vector)
@@ -178,7 +177,7 @@ def tile_picked_ykal_mean_po_kernel(
         ]
 
         def gather_ratio(t):
-            nc.vector.tensor_tensor(keep[t][:], picked(var_tables[t], track_list, 0, S), decay[t], ALU.mult)
+            nc.vector.tensor_tensor(ratio[t][:], picked(var_tables[t], track_list, 0, S), decay[t], ALU.mult)
 
         gather_ratio(0)
         multiply_tiles(y_banks[:PAIR], quantise_pair("w1_00", w1_first_pair), 0)
@@ -186,11 +185,21 @@ def tile_picked_ykal_mean_po_kernel(
         for t in range(1, PACK):
             gather_ratio(t)
 
-        def finish_keep(t):
-            nc.scalar.activation(roots[t], keep[t][:], ACT.Abs_reciprocal_sqrt, scale=ROOT_UNIT**2, bias=ROOT_UNIT**2)
-            nc.scalar.activation(keep[t][:], roots[t], ACT.Square, scale=ROOT_UNIT)
+        keep = []
 
-        kept_mean = [sb("kept_mean%d" % t, [P, S], F32) for t in range(LAST)] + [keep[LAST - 1]]
+        def take_root(t):
+            nc.scalar.activation(decay[t], ratio[t][:], ACT.Abs_reciprocal_sqrt, scale=ROOT_UNIT**2, bias=ROOT_UNIT**2)
+
+        def square_root_of(t, tag):
+            keep.append(sb("keep%d" % t, [P, S], F32, tag))
+            nc.scalar.activation(keep[t][:], decay[t], ACT.Square, scale=ROOT_UNIT)
+
+        take_root(0)
+        for t in range(LAST):
+            take_root(t + 1)
+            square_root_of(t, "var%d" % (t + 1))
+
+        kept_mean = [sb("kept_mean%d" % t, [P, S], F32)[:] for t in range(PAIR)]
 
         def gather_kept_mean(t, first, last):
             nc.vector.tensor_tensor(
@@ -200,13 +209,19 @@ def tile_picked_ykal_mean_po_kernel(
                 ALU.mult,
             )
 
-        for t in range(PAIR):
-            finish_keep(t)
         gather_kept_mean(0, 0, S)
         w1_first_pair = round_pair("w1_1", w1_raw[1], 0, negate_on_vector, 2)
         w1_second_pair = round_pair("w1_1", w1_raw[1], PAIR, negate_on_scalar)
-        for t in range(PAIR, PACK):
-            finish_keep(t)
+        square_root_of(LAST, "w1_1")
+        picked_mean = {t: sb("picked_mean%d" % t, [P, S], F32) for t in range(PAIR, PACK)}
+        nc.scalar.activation(picked_mean[2][:], picked(mean_tables[2], track_list, 0, S), ACT.Copy)
+        for first, last in spans:
+            nc.scalar.activation(
+                picked_mean[LAST][:, first:last], picked(mean_tables[LAST], track_list, first, last), ACT.Copy
+            )
+        late_rows = sb("late_rows", [P, LAST * S], F32, "mean3")
+        kept_mean.extend([late_rows[:, t * S : (t + 1) * S] for t in range(PAIR)])
+        turned_sums = [late_rows[:, PAIR * S + first : PAIR * S + last] for first, last in spans]
         multiply_tiles(y_banks[:PAIR], quantise_pair("w1_10", w1_first_pair, None, [0, 2, 1, 3]), 1)
         gather_kept_mean(1, 0, S)
 
@@ -239,8 +254,8 @@ def tile_picked_ykal_mean_po_kernel(
                             stop=(n == 1 and b == blocks - 1),
                             is_transpose=True,
                         )
-                turned_sum = sb("turned_sum%d" % h, [P, HALF], F32)
-                nc.scalar.copy(turned_sum[:], turned[:])
+                turned_sum = turned_sums[h]
+                nc.scalar.copy(turned_sum, turned[:])
                 upright = psum.tile([P, HALF], F32, name="upright%d" % h, tag="bank%d" % (3 + h))
                 for b in range(blocks):
                     cols = slice(b * P, (b + 1) * P)
@@ -248,7 +263,7 @@ def tile_picked_ykal_mean_po_kernel(
                 sums.append(upright)
             return sums
 
-        results = [sb("result0", [P, PACK, HALF], F32)]
+        results = [sb("result%d" % h, [P, PACK, HALF], F32) for h in range(2)]
 
         def add_terms(engine, t, h, first=0, last=HALF):
             cols = slice(h * HALF + first, h * HALF + last)
@@ -266,24 +281,25 @@ def tile_picked_ykal_mean_po_kernel(
         multiply_tiles(y_banks[PAIR:], quantise_pair("w1_11", w1_second_pair), 1)
         for t, h in ((0, 0), (1, 0), (1, 1), (0, 1)):
             weigh_y(t, h)
-        add_terms(nc.gpsimd, 0, 0)
+        for h in range(2):
+            add_terms(nc.gpsimd, 0, h)
         first_sums = add_on_tensor(1)
-        gather_kept_mean(2, 0, S)
-        results.append(sb("result1", [P, PACK, HALF], F32, "mean2"))
-        add_terms(nc.gpsimd, 0, 1)
         for h in range(2):
             nc.scalar.copy(results[h][:, 1, :], first_sums[h][:])
             store_rows(0, PAIR, h)
         for t in range(PAIR, PACK):
-            for h in range(2):
-                weigh_y(t, h)
+            nc.vector.scalar_tensor_tensor(weighted_y[t][:], keep[t][:], 1.0, y_banks[t][:], ALU.subtract, ALU.mult)
 
-        gather_kept_mean(LAST, 0, HALF)
-        for t in range(PAIR, PACK):
+        def weigh_mean(t, cols):
+            nc.vector.tensor_tensor(kept_mean[t][:, cols], picked_mean[t][:, cols], keep[t][:, cols], ALU.mult)
+
+        weigh_mean(LAST, halves[0])
+        weigh_mean(2, slice(0, S))
+        for t in (LAST, 2):
             add_terms(nc.vector, t, 0)
         store_rows(PAIR, PACK, 0)
         round_columns(nc.scalar.copy, 0, 0, HALF)
-        gather_kept_mean(LAST, HALF, S)
+        weigh_mean(LAST, halves[1])
         for first, last in ((0, VECTOR_COLUMNS), (VECTOR_COLUMNS, HALF)):
             for t in range(PAIR, PACK):
                 add_terms(nc.vector, t, 1, first, last)

@@ -198,6 +198,7 @@ def tile_picked_ykal_mean_po_kernel(
         for t in range(LAST):
             take_root(t + 1)
             square_root_of(t, "var%d" % (t + 1))
+        square_root_of(LAST, None)
 
         kept_mean = [sb("kept_mean%d" % t, [P, S], F32)[:] for t in range(PAIR)]
 
@@ -212,7 +213,6 @@ def tile_picked_ykal_mean_po_kernel(
         gather_kept_mean(0, 0, S)
         w1_first_pair = round_pair("w1_1", w1_raw[1], 0, negate_on_vector, 2)
         w1_second_pair = round_pair("w1_1", w1_raw[1], PAIR, negate_on_scalar)
-        square_root_of(LAST, "w1_1")
         picked_mean = {t: sb("picked_mean%d" % t, [P, S], F32) for t in range(PAIR, PACK)}
         nc.scalar.activation(picked_mean[2][:], picked(mean_tables[2], track_list, 0, S), ACT.Copy)
         for first, last in spans:
@@ -283,10 +283,11 @@ def tile_picked_ykal_mean_po_kernel(
             weigh_y(t, h)
         for h in range(2):
             add_terms(nc.gpsimd, 0, h)
+            store_rows(0, 1, h)
         first_sums = add_on_tensor(1)
         for h in range(2):
             nc.scalar.copy(results[h][:, 1, :], first_sums[h][:])
-            store_rows(0, PAIR, h)
+            store_rows(1, PAIR, h)
         for t in range(PAIR, PACK):
             nc.vector.scalar_tensor_tensor(weighted_y[t][:], keep[t][:], 1.0, y_banks[t][:], ALU.subtract, ALU.mult)
 

@@ -85,18 +85,14 @@ def tile_picked_ykal_mean_po_kernel(
         w1_raw = [load_weight(w1, "w1_0", 0)]
         nc.sync.dma_start(track_list[:], track)
         var_tables = [load_row_tile(var, "var", t) for t in range(PACK)]
-        mean_tables = [load_row_tile(mean, "mean", 0)]
         w1_raw.append(load_weight(w1, "w1_1", 1))
-        mean_tables.extend([load_row_tile(mean, "mean", t) for t in range(1, PACK)])
+        mean_tables = [load_row_tile(mean, "mean", t) for t in range(PACK)]
 
         identity = sb("identity", [P, P], F32)
         make_identity(nc, identity[:])
 
         def negate_on_vector(dst, src):
             nc.vector.tensor_scalar(dst, src, -1.0, None, ALU.mult)
-
-        def negate_on_scalar(dst, src):
-            nc.scalar.activation(dst, src, ACT.Copy, scale=-1.0)
 
         x_codes = [sb("xg%d" % g, [P, S], U32) for g in range(PASSES)]
         nc.vector.tensor_copy(x_codes[0][:], picked(word_table_0, offs_list, 0, S))
@@ -184,6 +180,10 @@ def tile_picked_ykal_mean_po_kernel(
         multiply_tiles(y_banks[PAIR:], quantise_pair("w1_01", w1_second_pair), 0)
         for t in range(1, PACK):
             gather_ratio(t)
+        w1_first_pair = round_pair("w1_1", w1_raw[1], 0, negate_on_vector)
+        w1_second_pair = round_pair("w1_1", w1_raw[1], PAIR, negate_on_vector)
+        multiply_tiles(y_banks[:PAIR], quantise_pair("w1_10", w1_first_pair, None, [0, 1]), 1)
+        multiply_tiles(y_banks[PAIR:], quantise_pair("w1_11", w1_second_pair), 1)
 
         keep = []
 
@@ -210,20 +210,16 @@ def tile_picked_ykal_mean_po_kernel(
                 ALU.mult,
             )
 
+        picked_mean = {t: sb("picked_mean%d" % t, [P, S], F32) for t in range(1, PACK)}
+
+        def gather_mean(t, first, last):
+            nc.scalar.activation(picked_mean[t][:, first:last], picked(mean_tables[t], track_list, first, last), ACT.Copy)
+
         gather_kept_mean(0, 0, S)
-        w1_first_pair = round_pair("w1_1", w1_raw[1], 0, negate_on_vector, 2)
-        w1_second_pair = round_pair("w1_1", w1_raw[1], PAIR, negate_on_scalar)
-        picked_mean = {t: sb("picked_mean%d" % t, [P, S], F32) for t in range(PAIR, PACK)}
-        nc.scalar.activation(picked_mean[2][:], picked(mean_tables[2], track_list, 0, S), ACT.Copy)
+        gather_mean(1, 0, S)
+        gather_mean(2, 0, S)
         for first, last in spans:
-            nc.scalar.activation(
-                picked_mean[LAST][:, first:last], picked(mean_tables[LAST], track_list, first, last), ACT.Copy
-            )
-        late_rows = sb("late_rows", [P, LAST * S], F32, "mean3")
-        kept_mean.extend([late_rows[:, t * S : (t + 1) * S] for t in range(PAIR)])
-        turned_sums = [late_rows[:, PAIR * S + first : PAIR * S + last] for first, last in spans]
-        multiply_tiles(y_banks[:PAIR], quantise_pair("w1_10", w1_first_pair, None, [0, 2, 1, 3]), 1)
-        gather_kept_mean(1, 0, S)
+            gather_mean(LAST, first, last)
 
         out_rows = out_0.rearrange("(p t) s -> p t s", t=PACK)
         out_words = out_1[0].rearrange("p c r -> p (c r)").bitcast(I32)
@@ -231,13 +227,7 @@ def tile_picked_ykal_mean_po_kernel(
         result_scales = sb("result_scales", [P, S], U8)
         halves = [slice(first, last) for first, last in spans]
         rounded_results = [sb("result_bf16_%d" % h, [P, HALF, PACK], BF16) for h in range(2)]
-        weighted_y = [sb("weighted_y%d" % t, [P, S], F32) for t in range(PACK)]
-
-        def weigh_y(t, h):
-            cols = halves[h]
-            nc.vector.scalar_tensor_tensor(
-                weighted_y[t][:, cols], keep[t][:, cols], 1.0, y_banks[t][:, cols], ALU.subtract, ALU.mult
-            )
+        weighted_y = {t: sb("weighted_y%d" % t, [P, S], F32)[:] for t in range(PACK)}
 
         def add_on_tensor(t):
             blocks = HALF // P
@@ -278,22 +268,25 @@ def tile_picked_ykal_mean_po_kernel(
             src = results[h][:].rearrange("p t (c i) -> p c t i", i=4)
             copy(dst[:, first // 4 : last // 4], src[:, first // 4 : last // 4])
 
-        multiply_tiles(y_banks[PAIR:], quantise_pair("w1_11", w1_second_pair), 1)
-        for t, h in ((0, 0), (1, 0), (1, 1), (0, 1)):
-            weigh_y(t, h)
-        for h in range(2):
-            add_terms(nc.gpsimd, 0, h)
-            store_rows(0, 1, h)
-        first_sums = add_on_tensor(1)
-        for h in range(2):
-            nc.scalar.copy(results[h][:, 1, :], first_sums[h][:])
-            store_rows(1, PAIR, h)
-        for t in range(PAIR, PACK):
-            nc.vector.scalar_tensor_tensor(weighted_y[t][:], keep[t][:], 1.0, y_banks[t][:], ALU.subtract, ALU.mult)
+        def weigh_whole_y(t):
+            nc.vector.scalar_tensor_tensor(weighted_y[t], keep[t][:], 1.0, y_banks[t][:], ALU.subtract, ALU.mult)
 
         def weigh_mean(t, cols):
             nc.vector.tensor_tensor(kept_mean[t][:, cols], picked_mean[t][:, cols], keep[t][:, cols], ALU.mult)
 
+        for t in range(PACK):
+            weigh_whole_y(t)
+        nc.gpsimd.tensor_tensor(kept_mean[1], picked_mean[1][:], keep[1][:], ALU.mult)
+        for h in range(2):
+            add_terms(nc.vector, 1, h)
+            store_rows(1, PAIR, h)
+        late_rows = sb("late_rows", [P, LAST * S], F32, "mean3")
+        kept_mean.extend([late_rows[:, t * S : (t + 1) * S] for t in range(PAIR)])
+        turned_sums = [late_rows[:, PAIR * S + first : PAIR * S + last] for first, last in spans]
+        first_sums = add_on_tensor(0)
+        for h in range(2):
+            nc.scalar.copy(results[h][:, 0, :], first_sums[h][:])
+            store_rows(0, 1, h)
         weigh_mean(LAST, halves[0])
         weigh_mean(2, slice(0, S))
         for t in (LAST, 2):

@@ -182,7 +182,7 @@ def tile_picked_ykal_mean_po_kernel(
             gather_ratio(t)
         w1_first_pair = round_pair("w1_1", w1_raw[1], 0, negate_on_vector)
         w1_second_pair = round_pair("w1_1", w1_raw[1], PAIR, negate_on_vector)
-        multiply_tiles(y_banks[:PAIR], quantise_pair("w1_10", w1_first_pair, None, [0, 1]), 1)
+        multiply_tiles(y_banks[:PAIR], quantise_pair("w1_10", w1_first_pair), 1)
         multiply_tiles(y_banks[PAIR:], quantise_pair("w1_11", w1_second_pair), 1)
 
         keep = []
@@ -287,13 +287,14 @@ def tile_picked_ykal_mean_po_kernel(
         for h in range(2):
             nc.scalar.copy(results[h][:, 0, :], first_sums[h][:])
             store_rows(0, 1, h)
-        weigh_mean(LAST, halves[0])
-        weigh_mean(2, slice(0, S))
+        for t in (LAST, 2):
+            weigh_mean(t, halves[0])
         for t in (LAST, 2):
             add_terms(nc.vector, t, 0)
         store_rows(PAIR, PACK, 0)
         round_columns(nc.scalar.copy, 0, 0, HALF)
-        weigh_mean(LAST, halves[1])
+        for t in (LAST, 2):
+            weigh_mean(t, halves[1])
         for first, last in ((0, VECTOR_COLUMNS), (VECTOR_COLUMNS, HALF)):
             for t in range(PAIR, PACK):
                 add_terms(nc.vector, t, 1, first, last)

@@ -95,9 +95,11 @@ def tile_picked_ykal_mean_po_kernel(
             nc.vector.tensor_scalar(dst, src, -1.0, None, ALU.mult)
 
         x_codes = [sb("xg%d" % g, [P, S], U32) for g in range(PASSES)]
-        nc.vector.tensor_copy(x_codes[0][:], picked(word_table_0, offs_list, 0, S))
+        for first in range(0, S, P):
+            nc.vector.tensor_copy(x_codes[0][:, first : first + P], picked(word_table_0, offs_list, first, first + P))
         x_scale_bytes = sb("xsg", [P, S], U8)
-        nc.vector.tensor_copy(x_scale_bytes[:], picked(x_scale_table, offs_list, 0, S))
+        for first in range(0, S, P):
+            nc.vector.tensor_copy(x_scale_bytes[:, first : first + P], picked(x_scale_table, offs_list, first, first + P))
 
         def round_pair(name, raw, t0, copy, calls=1):
             rounded = sb("%s_bf16_%d" % (name, t0), [P, PAIR * P * PACK], BF16)
@@ -142,7 +144,7 @@ def tile_picked_ykal_mean_po_kernel(
         z_halves = [psum.tile([P, HALF], F32, name="zh%d" % h, tag="bank%d" % h) for h in range(2)]
         z_others = [psum.tile([P, S], F32, name="z%d" % t, tag="bank%d" % (t + 1)) for t in range(1, PACK)]
 
-        w2_first_pair = round_pair("w2_0", w2_raw[0], 0, nc.vector.tensor_copy)
+        w2_first_pair = round_pair("w2_0", w2_raw[0], 0, nc.vector.tensor_copy, 16)
         w2_second_pair = round_pair("w2_0", w2_raw[0], PAIR, nc.scalar.copy)
         first_codes = sb("w2_0_codes", [P, PACK * P], U32, "xs")
         w2_pass = quantise_pair("w2_00", w2_first_pair, first_codes[:, : PAIR * P])

@@ -23,7 +23,6 @@ PASSES = K // K_PASS
 QUADRANTS = 4
 LIST_ROWS = 16
 PAIR = 2
-BANKS = 8
 HALF = S // 2
 LAST = PACK - 1
 ROOT_UNIT = 2.0**-16
@@ -95,19 +94,18 @@ def tile_picked_ykal_mean_po_kernel(
             nc.vector.tensor_scalar(dst, src, -1.0, None, ALU.mult)
 
         x_codes = [sb("xg%d" % g, [P, S], U32) for g in range(PASSES)]
-        for first in range(0, S, P):
-            nc.vector.tensor_copy(x_codes[0][:, first : first + P], picked(word_table_0, offs_list, first, first + P))
+        nc.vector.tensor_copy(x_codes[0][:], picked(word_table_0, offs_list, 0, S))
         x_scale_bytes = sb("xsg", [P, S], U8)
-        for first in range(0, S, P):
-            nc.vector.tensor_copy(x_scale_bytes[:, first : first + P], picked(x_scale_table, offs_list, first, first + P))
+        nc.vector.tensor_copy(x_scale_bytes[:], picked(x_scale_table, offs_list, 0, S))
 
-        def round_pair(name, raw, t0, copy, calls=1):
+        def round_pair(name, raw, t0, copies):
             rounded = sb("%s_bf16_%d" % (name, t0), [P, PAIR * P * PACK], BF16)
             dst = rounded[:].rearrange("p (t c j) -> p c j t", t=PAIR, j=PACK)
             src = raw[:].rearrange("p j (c t) -> p c j t", t=PACK)[:, :, :, t0 : t0 + PAIR]
-            width = P // calls
-            for first in range(0, P, width):
-                copy(dst[:, first : first + width], src[:, first : first + width])
+            width = P // len(copies)
+            for piece, copy in enumerate(copies):
+                rows = slice(piece * width, (piece + 1) * width)
+                copy(dst[:, rows], src[:, rows])
             return rounded
 
         def quantise_pair(name, rounded, codes=None, order=None):
@@ -141,38 +139,33 @@ def tile_picked_ykal_mean_po_kernel(
                 multiply(bank, tile_weights, g)
 
         spans = [(h * HALF, (h + 1) * HALF) for h in range(2)]
-        z_halves = [psum.tile([P, HALF], F32, name="zh%d" % h, tag="bank%d" % h) for h in range(2)]
-        z_others = [psum.tile([P, S], F32, name="z%d" % t, tag="bank%d" % (t + 1)) for t in range(1, PACK)]
+        z_banks = [
+            [psum.tile([P, HALF], F32, name="z%d_%d" % (h, t), tag="bank%d" % (PACK * h + t)) for t in range(PACK)]
+            for h in range(2)
+        ]
 
-        w2_first_pair = round_pair("w2_0", w2_raw[0], 0, nc.vector.tensor_copy, 16)
-        w2_second_pair = round_pair("w2_0", w2_raw[0], PAIR, nc.scalar.copy)
+        w2_first_pair = round_pair("w2_0", w2_raw[0], 0, [nc.vector.tensor_copy])
+        w2_second_pair = round_pair("w2_0", w2_raw[0], PAIR, [nc.scalar.copy])
         first_codes = sb("w2_0_codes", [P, PACK * P], U32, "xs")
         w2_pass = quantise_pair("w2_00", w2_first_pair, first_codes[:, : PAIR * P])
         w2_pass = w2_pass + quantise_pair("w2_01", w2_second_pair, first_codes[:, PAIR * P :])
-        for bank, (first, last) in zip(z_halves, spans):
-            multiply(bank, w2_pass[0], 0, first, last)
-        multiply_tiles(z_others, w2_pass[1:], 0)
+        for t in range(PACK):
+            for h, (first, last) in enumerate(spans):
+                multiply(z_banks[h][t], w2_pass[t], 0, first, last)
 
-        w2_first_pair = round_pair("w2_1", w2_raw[1], 0, nc.vector.tensor_copy)
-        w2_second_pair = round_pair("w2_1", w2_raw[1], PAIR, nc.scalar.copy)
-        w2_pass = quantise_pair("w2_10", w2_first_pair)
-        for bank, (first, last) in zip(z_halves, spans):
-            nc.vector.tensor_copy(x_codes[1][:, first:last], picked(word_table_1, offs_list, first, last))
-            multiply(bank, w2_pass[0], 1, first, last)
-        w2_pass = w2_pass + quantise_pair("w2_11", w2_second_pair)
-        multiply_tiles(z_others, w2_pass[1:], 1)
-
+        w2_first_pair = round_pair("w2_1", w2_raw[1], 0, [nc.vector.tensor_copy])
+        w2_second_pair = round_pair("w2_1", w2_raw[1], PAIR, [nc.scalar.copy])
+        w2_pass = quantise_pair("w2_10", w2_first_pair) + quantise_pair("w2_11", w2_second_pair)
         decay = [sb("decay%d" % t, [P, S], F32)[:] for t in range(PACK)]
         ratio = [sb("ratio%d" % t, [P, S], F32) for t in range(PACK)]
-        for bank, (first, last) in zip(z_halves, spans):
-            nc.scalar.activation(decay[0][:, first:last], bank[:], ACT.Exp, scale=-1.0)
-        w1_first_pair = round_pair("w1_0", w1_raw[0], 0, negate_on_vector)
-        w1_second_pair = round_pair("w1_0", w1_raw[0], PAIR, negate_on_vector)
-        for t in range(1, PACK):
-            nc.scalar.activation(decay[t], z_others[t - 1][:], ACT.Exp, scale=-1.0)
-        y_banks = [
-            psum.tile([P, S], F32, name="y%d" % t, tag="bank%d" % ((PACK + 1 + t) % BANKS)) for t in range(PACK)
-        ]
+        for h, (first, last) in enumerate(spans):
+            nc.vector.tensor_copy(x_codes[1][:, first:last], picked(word_table_1, offs_list, first, last))
+            for t in range(PACK):
+                multiply(z_banks[h][t], w2_pass[t], 1, first, last)
+                nc.scalar.activation(decay[t][:, first:last], z_banks[h][t][:], ACT.Exp, scale=-1.0)
+        w1_first_pair = round_pair("w1_0", w1_raw[0], 0, [negate_on_vector])
+        w1_second_pair = round_pair("w1_0", w1_raw[0], PAIR, [negate_on_vector])
+        y_banks = [psum.tile([P, S], F32, name="y%d" % t, tag="bank%d" % t) for t in range(PACK)]
 
         def gather_ratio(t):
             nc.vector.tensor_tensor(ratio[t][:], picked(var_tables[t], track_list, 0, S), decay[t], ALU.mult)
@@ -182,8 +175,8 @@ def tile_picked_ykal_mean_po_kernel(
         multiply_tiles(y_banks[PAIR:], quantise_pair("w1_01", w1_second_pair), 0)
         for t in range(1, PACK):
             gather_ratio(t)
-        w1_first_pair = round_pair("w1_1", w1_raw[1], 0, negate_on_vector)
-        w1_second_pair = round_pair("w1_1", w1_raw[1], PAIR, negate_on_vector)
+        w1_first_pair = round_pair("w1_1", w1_raw[1], 0, [negate_on_vector])
+        w1_second_pair = round_pair("w1_1", w1_raw[1], PAIR, [negate_on_vector])
         multiply_tiles(y_banks[:PAIR], quantise_pair("w1_10", w1_first_pair), 1)
         multiply_tiles(y_banks[PAIR:], quantise_pair("w1_11", w1_second_pair), 1)
 
@@ -235,7 +228,7 @@ def tile_picked_ykal_mean_po_kernel(
             blocks = HALF // P
             sums = []
             for h, (first, last) in enumerate(spans):
-                turned = psum.tile([P, HALF], F32, name="turned%d" % h, tag="bank%d" % (1 + h))
+                turned = psum.tile([P, HALF], F32, name="turned%d" % h, tag="bank%d" % (PACK + h))
                 for n, term in enumerate((kept_mean[t], weighted_y[t])):
                     for b in range(blocks):
                         nc.tensor.matmul(
@@ -248,7 +241,7 @@ def tile_picked_ykal_mean_po_kernel(
                         )
                 turned_sum = turned_sums[h]
                 nc.scalar.copy(turned_sum, turned[:])
-                upright = psum.tile([P, HALF], F32, name="upright%d" % h, tag="bank%d" % (3 + h))
+                upright = psum.tile([P, HALF], F32, name="upright%d" % h, tag="bank%d" % (PACK + 2 + h))
                 for b in range(blocks):
                     cols = slice(b * P, (b + 1) * P)
                     nc.tensor.transpose(upright[:, cols], turned_sum[:, cols], identity[:])

from contextlib import ExitStack

import concourse.mybir as mybir
from concourse.masks import make_identity

K, T, S, N, U = 1024, 1024, 512, 512, 1024
FLOPS = 2 * 2 * K * N * S

F32 = mybir.dt.float32
BF16 = mybir.dt.bfloat16
I32 = mybir.dt.int32
U32 = mybir.dt.uint32
U16 = mybir.dt.uint16
U8 = mybir.dt.uint8
FP8X4 = mybir.dt.float8_e4m3fn_x4
ACT = mybir.ActivationFunctionType
ALU = mybir.AluOpType

P = 128
PACK = 4
K_PASS = P * PACK
PASSES = K // K_PASS
QUADRANTS = 4
LIST_ROWS = 16
PAIR = 2
HALF = S // 2
LAST = PACK - 1
ROOT_UNIT = 2.0**-16
VECTOR_COLUMNS = 192
EARLY_SCALE_LOADS = 2


def tile_picked_ykal_mean_po_kernel(
    tc, x_words, x_scales, mean, var, w1, w2, offs, track, out_0, out_1, out_2
):
    nc = tc.nc
    with ExitStack() as ctx:
        sbuf = ctx.enter_context(tc.tile_pool(name="keep", bufs=1))
        psum = ctx.enter_context(tc.psum_pool(name="psum", bufs=1))

        def sb(name, shape, dtype, tag=None):
            return sbuf.tile(shape, dtype, name=name, tag=tag or name, align_bytes=64)

        offs_list = sbuf.tile([P, S // LIST_ROWS], U16, name="offs_t")
        track_list = sbuf.tile([P, S // LIST_ROWS], U16, name="track_t")

        def picked(table, entries, first, last):
            return table[:].indirect(entries[:, first // LIST_ROWS : last // LIST_ROWS])

        x_scale_table = sb("xs", [P, T], U8)
        nc.vector.memset(x_scale_table[:].bitcast(I32), 0)

        def load_words(g):
            table = sb("xw%d" % g, [P, T], U32)
            nc.sync.dma_start(table[:].bitcast(I32), x_words[g].rearrange("p n t -> p (n t)").bitcast(I32))
            return table

        def load_weight(w, name, g):
            raw = sb(name, [P, PACK, N], F32)
            nc.sync.dma_start(raw[:], w[g * K_PASS : (g + 1) * K_PASS, :].rearrange("(p j) n -> p j n", j=PACK))
            return raw

        def load_row_tile(src, name, t):
            table = sb("%s%d" % (name, t), [P, U], F32)
            nc.sync.dma_start(table[:], src.rearrange("(p t) u -> p t u", t=PACK)[:, t, :])
            return table

        def load_scale_rows(g, row):
            nc.sync.dma_start(
                x_scale_table[4 * g + row : P : 32, :].bitcast(I32),
                x_scales[g, row : 4 * QUADRANTS : 4, :].bitcast(I32),
            )

        scale_loads = [(g, row) for row in range(4) for g in range(PASSES)]
        word_table_0 = load_words(0)
        nc.sync.dma_start(offs_list[:], offs)
        for g, row in scale_loads[:EARLY_SCALE_LOADS]:
            load_scale_rows(g, row)
        w2_raw = [load_weight(w2, "w2_0", 0)]
        for g, row in scale_loads[EARLY_SCALE_LOADS:]:
            load_scale_rows(g, row)
        w2_raw.append(load_weight(w2, "w2_1", 1))
        word_table_1 = load_words(1)
        w1_raw = [load_weight(w1, "w1_0", 0)]
        nc.sync.dma_start(track_list[:], track)
        var_tables = [load_row_tile(var, "var", t) for t in range(PACK)]
        w1_raw.append(load_weight(w1, "w1_1", 1))
        mean_tables = [load_row_tile(mean, "mean", t) for t in range(PACK)]

        identity = sb("identity", [P, P], F32)
        make_identity(nc, identity[:])

        def negate_on_vector(dst, src):
            nc.vector.tensor_scalar(dst, src, -1.0, None, ALU.mult)

        x_codes = [sb("xg%d" % g, [P, S], U32) for g in range(PASSES)]
        nc.vector.tensor_copy(x_codes[0][:], picked(word_table_0, offs_list, 0, S))
        x_scale_bytes = sb("xsg", [P, S], U8)
        nc.vector.tensor_copy(x_scale_bytes[:], picked(x_scale_table, offs_list, 0, S))

        def round_pair(name, raw, t0, copies):
            rounded = sb("%s_bf16_%d" % (name, t0), [P, PAIR * P * PACK], BF16)
            dst = rounded[:].rearrange("p (t c j) -> p c j t", t=PAIR, j=PACK)
            src = raw[:].rearrange("p j (c t) -> p c j t", t=PACK)[:, :, :, t0 : t0 + PAIR]
            width = P // len(copies)
            for piece, copy in enumerate(copies):
                rows = slice(piece * width, (piece + 1) * width)
                copy(dst[:, rows], src[:, rows])
            return rounded

        def quantise_pair(name, rounded, codes=None, order=None):
            if codes is None:
                codes = sb("%s_codes" % name, [P, PAIR * P], U32)[:]
            scales = sb("%s_scales" % name, [P, PAIR * P], U8)
            width = PAIR * P // len(order or [0])
            for piece in order or [0]:
                cols = slice(piece * width, (piece + 1) * width)
                nc.vector.quantize_mx(
                    out=codes[:, cols].bitcast(FP8X4),
                    scales=scales[:, cols],
                    in_=rounded[:, PACK * piece * width : PACK * (piece + 1) * width],
                )
            return [(codes[:, t * P : (t + 1) * P], scales[:, t * P : (t + 1) * P]) for t in range(PAIR)]

        def multiply(bank, tile_weights, g, first=0, last=S):
            codes, scales = tile_weights
            nc.tensor.matmul_mx(
                out=bank[:],
                lhsT=codes.bitcast(FP8X4),
                lhsT_scale=scales,
                rhs=x_codes[g][:, first:last].bitcast(FP8X4),
                rhs_scale=x_scale_bytes[4 * g : P, first:last],
                start=(g == 0),
                stop=(g == PASSES - 1),
            )

        def multiply_tiles(banks, weights, g):
            for bank, tile_weights in zip(banks, weights):
                multiply(bank, tile_weights, g)

        spans = [(h * HALF, (h + 1) * HALF) for h in range(2)]
        z_banks = [
            [psum.tile([P, HALF], F32, name="z%d_%d" % (h, t), tag="bank%d" % (PACK * h + t)) for t in range(PACK)]
            for h in range(2)
        ]

        w2_first_pair = round_pair("w2_0", w2_raw[0], 0, [nc.vector.tensor_copy])
        w2_second_pair = round_pair("w2_0", w2_raw[0], PAIR, [nc.scalar.copy])
        first_codes = sb("w2_0_codes", [P, PACK * P], U32, "xs")
        w2_pass = quantise_pair("w2_00", w2_first_pair, first_codes[:, : PAIR * P])
        w2_pass = w2_pass + quantise_pair("w2_01", w2_second_pair, first_codes[:, PAIR * P :])
        for t in range(PACK):
            for h, (first, last) in enumerate(spans):
                multiply(z_banks[h][t], w2_pass[t], 0, first, last)

        w2_first_pair = round_pair("w2_1", w2_raw[1], 0, [nc.vector.tensor_copy])
        w2_second_pair = round_pair("w2_1", w2_raw[1], PAIR, [nc.scalar.copy])
        w2_pass = quantise_pair("w2_10", w2_first_pair) + quantise_pair("w2_11", w2_second_pair)
        decay = [sb("decay%d" % t, [P, S], F32)[:] for t in range(PACK)]
        ratio = [sb("ratio%d" % t, [P, S], F32) for t in range(PACK)]
        for h, (first, last) in enumerate(spans):
            nc.vector.tensor_copy(x_codes[1][:, first:last], picked(word_table_1, offs_list, first, last))
            for t in range(PACK):
                multiply(z_banks[h][t], w2_pass[t], 1, first, last)
                nc.scalar.activation(decay[t][:, first:last], z_banks[h][t][:], ACT.Exp, scale=-1.0)
        w1_first_pair = round_pair("w1_0", w1_raw[0], 0, [negate_on_vector])
        w1_second_pair = round_pair("w1_0", w1_raw[0], PAIR, [negate_on_vector])
        y_banks = [psum.tile([P, S], F32, name="y%d" % t, tag="bank%d" % t) for t in range(PACK)]

        def gather_ratio(t):
            nc.vector.tensor_tensor(ratio[t][:], picked(var_tables[t], track_list, 0, S), decay[t], ALU.mult)

        gather_ratio(0)
        multiply_tiles(y_banks[:PAIR], quantise_pair("w1_00", w1_first_pair), 0)
        multiply_tiles(y_banks[PAIR:], quantise_pair("w1_01", w1_second_pair), 0)
        for t in range(1, PACK):
            gather_ratio(t)
        w1_first_pair = round_pair("w1_1", w1_raw[1], 0, [negate_on_vector])
        w1_second_pair = round_pair("w1_1", w1_raw[1], PAIR, [negate_on_vector])
        multiply_tiles(y_banks[:PAIR], quantise_pair("w1_10", w1_first_pair), 1)
        multiply_tiles(y_banks[PAIR:], quantise_pair("w1_11", w1_second_pair), 1)

        keep = []

        def take_root(t):
            nc.scalar.activation(decay[t], ratio[t][:], ACT.Abs_reciprocal_sqrt, scale=ROOT_UNIT**2, bias=ROOT_UNIT**2)

        def square_root_of(t, tag):
            keep.append(sb("keep%d" % t, [P, S], F32, tag))
            nc.scalar.activation(keep[t][:], decay[t], ACT.Square, scale=ROOT_UNIT)

        take_root(0)
        for t in range(LAST):
            take_root(t + 1)
            square_root_of(t, "var%d" % (t + 1))
        square_root_of(LAST, None)

        kept_mean = [sb("kept_mean%d" % t, [P, S], F32)[:] for t in range(PAIR)]

        def gather_kept_mean(t, first, last):
            nc.vector.tensor_tensor(
                kept_mean[t][:, first:last],
                picked(mean_tables[t], track_list, first, last),
                keep[t][:, first:last],
                ALU.mult,
            )

        picked_mean = {t: sb("picked_mean%d" % t, [P, S], F32) for t in range(1, PACK)}

        def gather_mean(t, first, last):
            nc.scalar.activation(picked_mean[t][:, first:last], picked(mean_tables[t], track_list, first, last), ACT.Copy)

        gather_kept_mean(0, 0, S)
        gather_mean(1, 0, S)
        gather_mean(2, 0, S)
        for first, last in spans:
            gather_mean(LAST, first, last)

        out_rows = out_0.rearrange("(p t) s -> p t s", t=PACK)
        out_words = out_1[0].rearrange("p c r -> p (c r)").bitcast(I32)
        result_codes = sb("result_codes", [P, S], U32)
        result_scales = sb("result_scales", [P, S], U8)
        halves = [slice(first, last) for first, last in spans]
        rounded_results = [sb("result_bf16_%d" % h, [P, HALF, PACK], BF16) for h in range(2)]
        weighted_y = {t: sb("weighted_y%d" % t, [P, S], F32)[:] for t in range(PACK)}

        def add_on_tensor(t):
            blocks = HALF // P
            sums = []
            for h, (first, last) in enumerate(spans):
                turned = psum.tile([P, HALF], F32, name="turned%d" % h, tag="bank%d" % (PACK + h))
                for n, term in enumerate((kept_mean[t], weighted_y[t])):
                    for b in range(blocks):
                        nc.tensor.matmul(
                            turned[:, b * P : (b + 1) * P],
                            term[:, first + b * P : first + (b + 1) * P],
                            identity[:],
                            start=(n == 0 and b == 0),
                            stop=(n == 1 and b == blocks - 1),
                            is_transpose=True,
                        )
                turned_sum = turned_sums[h]
                nc.scalar.copy(turned_sum, turned[:])
                upright = psum.tile([P, HALF], F32, name="upright%d" % h, tag="bank%d" % (PACK + 2 + h))
                for b in range(blocks):
                    cols = slice(b * P, (b + 1) * P)
                    nc.tensor.transpose(upright[:, cols], turned_sum[:, cols], identity[:])
                sums.append(upright)
            return sums

        results = [sb("result%d" % h, [P, PACK, HALF], F32) for h in range(2)]

        def add_terms(engine, t, h, first=0, last=HALF):
            cols = slice(h * HALF + first, h * HALF + last)
            engine.tensor_tensor(results[h][:, t, first:last], kept_mean[t][:, cols], weighted_y[t][:, cols], ALU.add)

        def store_rows(first_tile, last_tile, h):
            rows = slice(first_tile, last_tile)
            nc.sync.dma_start(out_rows[:, rows, halves[h]], results[h][:, rows, :])

        def round_columns(copy, h, first, last):
            dst = rounded_results[h][:].rearrange("p (c i) t -> p c t i", i=4)
            src = results[h][:].rearrange("p t (c i) -> p c t i", i=4)
            copy(dst[:, first // 4 : last // 4], src[:, first // 4 : last // 4])

        def weigh_whole_y(t):
            nc.vector.scalar_tensor_tensor(weighted_y[t], keep[t][:], 1.0, y_banks[t][:], ALU.subtract, ALU.mult)

        def weigh_mean(t, cols):
            nc.vector.tensor_tensor(kept_mean[t][:, cols], picked_mean[t][:, cols], keep[t][:, cols], ALU.mult)

        for t in range(PACK):
            weigh_whole_y(t)
        nc.gpsimd.tensor_tensor(kept_mean[1], picked_mean[1][:], keep[1][:], ALU.mult)
        for h in range(2):
            add_terms(nc.vector, 1, h)
            store_rows(1, PAIR, h)
        late_rows = sb("late_rows", [P, LAST * S], F32, "mean3")
        kept_mean.extend([late_rows[:, t * S : (t + 1) * S] for t in range(PAIR)])
        turned_sums = [late_rows[:, PAIR * S + first : PAIR * S + last] for first, last in spans]
        first_sums = add_on_tensor(0)
        for h in range(2):
            nc.scalar.copy(results[h][:, 0, :], first_sums[h][:])
            store_rows(0, 1, h)
        for t in (LAST, 2):
            weigh_mean(t, halves[0])
        for t in (LAST, 2):
            add_terms(nc.vector, t, 0)
        store_rows(PAIR, PACK, 0)
        round_columns(nc.scalar.copy, 0, 0, HALF)
        for t in (LAST, 2):
            weigh_mean(t, halves[1])
        for first, last in ((0, VECTOR_COLUMNS), (VECTOR_COLUMNS, HALF)):
            for t in range(PAIR, PACK):
                add_terms(nc.vector, t, 1, first, last)
        store_rows(PAIR, PACK, 1)
        round_columns(nc.vector.tensor_copy, 1, 0, VECTOR_COLUMNS)
        round_columns(nc.scalar.copy, 1, VECTOR_COLUMNS, HALF)

        for rounded, cols in zip(rounded_results, halves):
            nc.vector.quantize_mx(
                out=result_codes[:, cols].bitcast(FP8X4),
                scales=result_scales[:, cols],
                in_=rounded[:].rearrange("p c t -> p (c t)"),
            )
            nc.sync.dma_start(out_words[:, cols], result_codes[:, cols].bitcast(I32))
        for quad in range(QUADRANTS):
            engine = nc.sync if quad == QUADRANTS - 1 else nc.scalar
            engine.dma_start(
                out_2[0, 4 * quad : 4 * quad + 4, :].bitcast(I32),
                result_scales[32 * quad : 32 * quad + 4, :].bitcast(I32),
            )
